import numpy as np, ml_dtypes
CORES = [5,29,101,125,133,157,229,253]
N = 8
BF = ml_dtypes.bfloat16
def gentries(a):
    return np.ascontiguousarray(a.reshape(8, 16, -1).transpose(0, 2, 1)).reshape(8, -1)
def gtable(e):
    e = np.asarray(e); return np.ascontiguousarray(e.reshape(8, -1, 16).transpose(0, 2, 1)).reshape(128, -1).astype(np.int32)
W, n, V, C, Z = 6, 2048, 8192, 1024, 256
def counts(rng, h, z):
    c = np.zeros((N, 8, W), np.int64)
    for r in range(N):
        for g in range(8):
            m = int(h[r, g] - z[r, g]) - (W - 2); b = np.sort(rng.integers(0, m + 1, W - 3))
            c[r, g, 0] = n - h[r, g]; c[r, g, 1:W - 1] = np.diff(np.concatenate([[0], b, [m]])) + 1; c[r, g, W - 1] = z[r, g]
    return c
def some(rng):
    return rng.integers(C - C // 4, C + 1, (N, 8)), rng.integers(Z // 2, Z + 1, (N, 8))
def names(rng):
    return np.stack([np.stack([rng.permutation(V)[:n] for g in range(8)]) for r in range(N)]).astype(np.int64)
def depths(rng, c):
    return np.stack([np.stack([rng.permutation(np.repeat(np.arange(W), c[r, g])) for g in range(8)]) for r in range(N)])
def link(rng, o, dep):
    x = np.zeros((N, 8, n), np.int64)
    for r in range(N):
        q = (r + 1) % N
        for g in range(8):
            m = np.ones(V, bool); m[o[q, g]] = False; free = np.flatnonzero(m)
            v = free[rng.integers(0, len(free), n)]
            for k in range(1, W):
                i = np.flatnonzero(dep[r, g] == k)
                if len(i):
                    t = np.flatnonzero(dep[q, g] == k - 1 if k < W - 1 else dep[q, g] >= W - 2)
                    v[i] = o[q, g][t[rng.integers(0, len(t), len(i))]]
            x[r, g] = v
    return x
def pack(o, x, s):
    return {"own": np.stack([gtable(a) for a in o]), "nxt": np.stack([gtable(a) for a in x]), "pts": np.asarray(s).astype(np.int32)}
def points(rng):
    return rng.integers(0, 256, (N, 8, n))
def setup_inputs(rng):
    h, z = some(rng); o = names(rng); dep = depths(rng, counts(rng, h, z))
    return pack(o, link(rng, o, dep), points(rng))
def setup_inputs_full(rng):
    o = names(rng); c = counts(rng, np.full((N, 8), C), np.full((N, 8), Z)); e = rng.permutation(8)[:4]
    c[:, e, 1:W - 2] = 1; c[:, e, W - 2] = C - Z - (W - 3)
    dep = depths(rng, c)
    return pack(o, link(rng, o, dep), points(rng))
def setup_inputs_few(rng):
    h, z = some(rng); e = rng.permutation(8); q = int(rng.integers(0, N)); o = names(rng)
    z[:, e[2]] = 1; z[:, e[3]] = np.where(rng.random(N) < 0.5, 0, z[:, e[3]]); z[q, e[3]] = 0; z[:, e[4]] = Z; h[:, e[4]] = C
    c = counts(rng, h, z); c[:, e[0], 0] = n; c[:, e[0], 1:] = 0
    for t in range(W - 1):
        r = (q - t) % N; c[r, e[1], 0] += np.sum(c[r, e[1], t + 1:]); c[r, e[1], t + 1:] = 0
    dep = depths(rng, c)
    return pack(o, link(rng, o, dep), points(rng))
def setup_inputs_repeats(rng):
    h, z = some(rng); o = names(rng); dep = depths(rng, counts(rng, h, z)); x = link(rng, o, dep)
    for r in range(N):
        for g in range(8):
            for k in (0, W - 1):
                i = np.flatnonzero(dep[r, g] == k); x[r, g, i] = x[r, g, i[0]]
    return pack(o, x, points(rng))
def setup_inputs_ends(rng):
    h, z = some(rng); dep = depths(rng, counts(rng, h, z))
    o = 1 + np.stack([np.stack([rng.permutation(V - 2)[:n] for g in range(8)]) for r in range(N)]).astype(np.int64)
    for r in range(N):
        for g in range(0, 8, 2):
            o[r, g, 0] = 0; o[r, g, n - 1] = V - 1; a = dep[r, g]
            i = np.flatnonzero(a == W - 1); j = i[rng.integers(0, len(i))]; u, v = int(a[0]), int(a[j]); a[j] = u; a[0] = v
            i = np.flatnonzero(a[1:] == W - 1) + 1; j = i[rng.integers(0, len(i))]; u, v = int(a[n - 1]), int(a[j]); a[j] = u; a[n - 1] = v
    x = link(rng, o, dep)
    x[:, 0::2, 0] = V - 1; x[:, 0::2, n - 1] = 0
    for g in range(1, 8, 2):
        m = (dep[:, g] == 0) & (rng.random((N, n)) < 0.5)
        x[:, g] = np.where(m, rng.integers(0, 2, (N, n)) * (V - 1), x[:, g])
    return pack(o, x, 255 * rng.integers(0, 2, (N, 8, n)))
def setup_inputs_spread(rng):
    z = np.maximum(Z >> rng.integers(0, 7, (N, 8)), 1); h = z + np.maximum((C - Z) >> rng.integers(0, 7, (N, 8)), W - 2)
    o = np.stack([np.stack([(rng.integers(0, V) + rng.permutation(n + n // 8)[:n]) % V for g in range(8)]) for r in range(N)]).astype(np.int64)
    o[:, 1::2] = np.sort(o[:, 1::2], axis=2)
    dep = depths(rng, counts(rng, h, z))
    return pack(o, link(rng, o, dep), 255 >> rng.integers(0, 9, (N, 8, n)))
def followers(o, x):
    to = np.zeros((N, 8, n), np.int64)
    for r in range(N):
        for g in range(8):
            where = np.full(V, -1, np.int64); where[o[(r + 1) % N, g]] = np.arange(n); to[r, g] = where[x[r, g]]
    return to
def step(p, v, t):
    return np.take_along_axis(np.roll(v, -t, axis=0), p, axis=2)
def chains(to, s):
    p = np.broadcast_to(np.arange(n), (N, 8, n)); tot = s.astype(np.int64)
    for t in range(1, W):
        p = np.where(p >= 0, step(np.maximum(p, 0), to, t - 1), -1)
        tot = tot + np.where(p >= 0, step(np.maximum(p, 0), s, t), 0)
    return p, tot
def check_inputs(d):
    try:
        o = np.stack([gentries(a) for a in d["own"]]).astype(np.int64); x = np.stack([gentries(a) for a in d["nxt"]]).astype(np.int64); s = np.asarray(d["pts"]).astype(np.int64)
        if o.shape != (N, 8, n) or x.shape != (N, 8, n) or s.shape != (N, 8, n): return ["shapes"]
        bad = []
        if s.min() < 0 or s.max() > 255: bad.append("points")
        if o.min() < 0 or o.max() >= V or x.min() < 0 or x.max() >= V: return bad + ["names in range"]
        if (np.diff(np.sort(o, axis=2), axis=2) == 0).any(): return bad + ["own names differ"]
        to = followers(o, x); p, tot = chains(to, s)
        if np.max(np.count_nonzero(to >= 0, axis=2)) > C: bad.append("followers")
        if np.max(np.count_nonzero(p >= 0, axis=2)) > Z: bad.append("kept")
        return bad
    except Exception:
        return ["shapes"]
def reference(own, nxt, pts):
    o = np.stack([gentries(a) for a in own]).astype(np.int64); x = np.stack([gentries(a) for a in nxt]).astype(np.int64)
    p, tot = chains(followers(o, x), pts)
    yk = np.full((N, 8, Z), -1, np.float32); ys = np.zeros((N, 8, Z), np.float32)
    for r in range(N):
        for g in range(8):
            i = np.flatnonzero(p[r, g] >= 0)
            yk[r, g, :len(i)] = o[r, g, i]; ys[r, g, :len(i)] = tot[r, g, i]
    return {"yk": yk, "ys": ys}

@@ -1,0 +1,421 @@
+from concourse.bass import DstId, RemoteDMATransfer
+from concourse.mybir import AluOpType as OP, ActivationFunctionType as AF
+
+SCRATCH = {
+    "nx": ("sbuf", [128, 128], "uint16"),
+    "rln": ("sbuf", [128, 128], "uint16"), "rlf": ("sbuf", [128, 128], "uint16"), "rlp": ("sbuf", [128, 128], "bfloat16"),
+    "rlq": ("dram", [128, 128], "bfloat16"),
+    "owi": ("sbuf", [128, 128], "int32"), "nxi": ("sbuf", [128, 128], "int32"), "pti": ("sbuf", [128, 128], "int32"),
+    "own16": ("sbuf", [128, 128], "uint16"), "nxt16": ("sbuf", [128, 128], "uint16"), "pt0": ("sbuf", [128, 128], "bfloat16"),
+    "tab": ("sbuf", [128, 8192], "bfloat16"), "vr": ("sbuf", [128, 2048], "bfloat16"), "gr": ("sbuf", [128, 2048], "bfloat16"),
+    "f0": ("sbuf", [128, 128], "uint16"), "fg": ("sbuf", [128, 128], "uint16"),
+    "xs": ("dram", [128, 256], "bfloat16"), "xr": ("dram", [128, 256], "bfloat16"),
+    "xp": ("dram", [128, 128], "bfloat16"), "pq5": ("dram", [128, 128], "bfloat16"), "pq3": ("dram", [128, 128], "bfloat16"),
+    "xw": ("sbuf", [128, 2064], "bfloat16"), "xg": ("sbuf", [128, 2048], "bfloat16"),
+    "w5": ("sbuf", [128, 2064], "bfloat16"), "wd": ("sbuf", [128, 2064], "bfloat16"), "wb": ("sbuf", [128, 2064], "bfloat16"),
+    "d3": ("sbuf", [128, 512], "bfloat16"), "rr": ("sbuf", [128, 2048], "bfloat16"), "pr2": ("sbuf", [128, 2048], "bfloat16"),
+    "lo": ("sbuf", [128, 256], "bfloat16"), "m1": ("sbuf", [128, 256], "bfloat16"), "ip": ("sbuf", [128, 2], "int32"),
+    "io8": ("sbuf", [128, 8], "float32"), "pb": ("sbuf", [128, 1], "int32"),
+    "pg": ("sbuf", [128, 1], "int32"),
+    "ml": ("sbuf", [128, 1], "float32"), "nml": ("sbuf", [128, 1], "float32"), "hb": ("sbuf", [128, 8], "float32"),
+    "gf": ("sbuf", [128, 1], "float32"), "ngf": ("sbuf", [128, 1], "float32"),
+    "zz": ("sbuf", [128, 160], "bfloat16"), "on": ("sbuf", [128, 160], "bfloat16"), "half": ("sbuf", [128, 32], "bfloat16"),
+    "basef": ("sbuf", [128, 144], "bfloat16"), "bases": ("sbuf", [128, 144], "bfloat16"), "base0": ("sbuf", [128, 144], "bfloat16"),
+    "ids": ("sbuf", [128, 128], "bfloat16"),
+    "bo": ("sbuf", [128, 128], "bfloat16"), "tri": ("sbuf", [128, 128], "bfloat16"), "bo16": ("sbuf", [128, 128], "bfloat16"),
+    "boh": ("sbuf", [128, 8], "float16"), "kc": ("sbuf", [128, 128], "bfloat16"), "cp": ("sbuf", [128, 128], "bfloat16"),
+    "ck": ("sbuf", [128, 128], "bfloat16"), "msk": ("sbuf", [128, 32], "float32"),
+    "loi": ("sbuf", [128, 128], "int32"), "nlo": ("sbuf", [128, 144], "bfloat16"), "nhi": ("sbuf", [128, 144], "bfloat16"),
+    "kt": ("sbuf", [128, 128], "bfloat16"), "sc1": ("sbuf", [128, 144], "bfloat16"), "sumw": ("sbuf", [128, 144], "float32"),
+    "posk": ("sbuf", [128, 144], "bfloat16"), "ai": ("sbuf", [128, 128], "int32"), "a1": ("sbuf", [128, 128], "bfloat16"),
+    "bb": ("sbuf", [128, 128], "bfloat16"), "sg": ("sbuf", [128, 128], "bfloat16"), "cmm": ("sbuf", [128, 32], "float32"),
+    "lf": ("sbuf", [128, 16], "float32"), "lst": ("sbuf", [128, 16], "uint16"), "oh": ("sbuf", [128, 256], "bfloat16"),
+    "vs": ("sbuf", [128, 256], "float16"), "vh": ("sbuf", [128, 256], "bfloat16"), "vl": ("sbuf", [128, 256], "bfloat16"),
+    "yks": ("sbuf", [128, 256], "float32"), "yss": ("sbuf", [128, 256], "float32"),
+    "psa": ("psum", [128, 2048], "float32"), "pwa": ("psum", [128, 512], "float32"), "pwb": ("psum", [128, 512], "float32"),
+    "px": ("psum", [128, 512], "float32"), "py": ("psum", [128, 512], "float32"),
+}
+for _k in (1, 3, 4):
+    SCRATCH["f%d" % _k] = ("sbuf", [128, 128], "uint16")
+for _k in (1, 2, 4):
+    SCRATCH["pt%d" % _k] = ("sbuf", [128, 128], "bfloat16")
+NTOK = 130
+SEMAPHORES = (["t%d" % _k for _k in range(NTOK)] + ["anx", "rn", "rf", "rp", "rq", "lc", "ax", "af1", "af3", "af4", "aq3", "aq5"]
+              + ["ap1", "ap2", "ap4"])
+
+ODD = (5, 3, 1)
+NONE = -2048
+
+
+def engs(topo, src, dst, a, b):
+    e = topo.engines(src, dst)[a:b]
+    return sum(1 << x for x in e), len(e)
+
+
+def write(g, T, topo, src, dst, out, in_, sem, a=0, b=8):
+    rid, pid = topo.addr(dst, src)
+    m, k = engs(topo, src, dst, a, b)
+    g.remote_dma(out, in_, T.sem[sem], T.sem["lc"], pid, rid, m)
+    return k
+
+
+def writes(g, T, topo, src, parts):
+    tr, n = [], 0
+    for dst, out, in_, sem, a, b in parts:
+        rid, pid = topo.addr(dst, src)
+        m, k = engs(topo, src, dst, a, b)
+        n += k
+        tr.append(RemoteDMATransfer(dst_ids=[DstId(rid=rid, pnc=pid)], dma_engine_mask=m, remote_sem=T.sem[sem], src=in_, dst=out))
+    g.remote_dma_fused(tr, local_sem=T.sem["lc"])
+    return n
+
+
+def helpers(T, topo, rc):
+    q, N = T.rank_of(rc), len(T.cores)
+    far = [T.cores[(q + 1) % N]] + [T.cores[(q - k) % N] for k in ODD]
+    c = [x for x in topo.cores_of(rc) if x != rc and topo.die(x) == topo.die(rc) and all(topo.may_write(x, d) for d in far)]
+    return c[0], c[1]
+
+
+def hand_on(g, core, T, topo):
+    N = len(T.cores)
+    for rc in T.cores:
+        if rc not in topo.cores_of(core):
+            continue
+        q = T.rank_of(rc)
+        A, B = helpers(T, topo, rc)
+        sent = 0
+        if core == A:
+            g.wait_ge(T.sem["rn"], 8)
+            sent += write(g, T, topo, core, T.cores[(q + 1) % N], T["nx"][:], T["rln"][:], "anx")
+            g.wait_ge(T.sem["rf"], 8)
+            sent += write(g, T, topo, core, T.cores[(q - 1) % N], T["f1"][:], T["rlf"][:], "af1")
+            sent += write(g, T, topo, core, T.cores[(q - 3) % N], T["f3"][:], T["rlf"][:], "af3")
+        elif core == B:
+            g.wait_ge(T.sem["rp"], 8)
+            sent += write(g, T, topo, core, T.cores[(q - 1) % N], T["pt1"][:], T["rlp"][:], "ap1")
+            g.wait_ge(T.sem["rq"], 4)
+            sent += write(g, T, topo, core, T.cores[(q - 5) % N], T["pq5"][:], T["rlq"][:], "aq5")
+            sent += write(g, T, topo, core, T.cores[(q - 3) % N], T["pq3"][:], T["rlq"][:], "aq3")
+        if sent:
+            g.wait_ge(T.sem["lc"], sent)
+
+
+def rank_program(g, core, T, topo):
+    q = T.rank_of(core)
+    if q is None:
+        hand_on(g, core, T, topo)
+        return
+    N = len(T.cores)
+    Q = {"g": g, "v": g.vector, "s": g.scalar, "t": g.tensor, "y": g.sync}
+    v, s, t = g.vector, g.scalar, g.tensor
+    used, seen = [0], {}
+    small = {"allow_small_or_imprecise_dtypes": True}
+
+    def tok():
+        used[0] += 1
+        return [T.sem["t%d" % (used[0] - 1)], 0, used[0] - 1]
+
+    def inc(op, k=None, n=1):
+        k = k or tok()
+        op.then_inc(k[0], n)
+        k[1] += n
+        return k
+
+    def W(queue, *toks):
+        for k in toks:
+            if seen.get((queue, k[2]), -1) < k[1]:
+                seen[(queue, k[2])] = k[1]
+                Q[queue].wait_ge(k[0], k[1])
+
+    def R(queue, sem, n):
+        if (queue, sem) not in seen:
+            seen[(queue, sem)] = n
+            Q[queue].wait_ge(T.sem[sem], n)
+
+    l_ow = inc(g.sync.dma_start(T["owi"][:], T.own[:]), None, 16)
+    l_nx = inc(g.scalar.dma_start(T["nxi"][:], T.nxt[:]), None, 16)
+    l_pt = inc(g.sync.dma_start(T["pti"][:], T.pts[:]), None, 16)
+
+    tab = T["tab"]
+    k_i = inc(g.iota(T["ip"][:, 0:1], [[0, 1]], 0, 1))
+    inc(g.iota(T["io8"][:], [[1, 8]], 0, 0, **small), k_i)
+    k_lo = inc(g.iota(T["lo"][:], [[1, 256]], 0, 0, **small))
+    k_fill = inc(g.iota(tab[:, 7168:8192], [[0, 1024]], NONE, 0, **small))
+
+    k_f0 = inc(v.memset(tab[:, 0:512], float(NONE)))
+    k_f1 = inc(v.memset(tab[:, 512:1024], float(NONE)))
+    W("y", k_f0, k_f1)
+    k_fd = inc(g.sync.dma_start(tab[:, 3840:4864], tab[:, 0:1024]), None, 16)
+    W("s", k_f0)
+    k_f2 = inc(s.activation(tab[:, 1024:1536], tab[:, 0:512], AF.Copy))
+    W("s", k_f1)
+    inc(s.activation(tab[:, 1536:2560], tab[:, 0:1024], AF.Copy), k_fill)
+    W("s", k_f2)
+    inc(s.activation(tab[:, 2560:3840], tab[:, 0:1280], AF.Copy), k_fill)
+
+    k_z = inc(v.memset(T["zz"][:], 0.0))
+    W("v", k_i)
+    k1 = inc(v.tensor_scalar(T["pb"][:], T["ip"][:, 0:1], 3, 1, OP.arith_shift_right, OP.bitwise_and))
+    W("v", k1)
+    k2 = inc(v.tensor_copy(T["ml"][:], T["pb"][:]))
+    k3 = inc(v.tensor_scalar(T["nml"][:], T["pb"][:], -1.0, 1.0, OP.mult, OP.add))
+    W("v", k3)
+    inc(v.tensor_scalar(T["hb"][:], T["io8"][:], T["nml"][:, 0:1], None, OP.mult), k2)
+    W("v", k2, k_lo)
+    k_vr = tok()
+    for b in range(8):
+        inc(v.tensor_scalar(T["vr"][:, 256 * b:256 * b + 256], T["lo"][:], T["ml"][:, 0:1], T["hb"][:, b:b + 1], OP.mult, OP.add), k_vr)
+    W("v", l_pt)
+    k_p0 = inc(v.tensor_copy(T["pt0"][:], T["pti"][:]))
+    W("y", k_vr, k_p0)
+    k_vp = inc(g.sync.dma_start(T["vr"][4:128:16, :], T["pt0"][:]), None, 16)
+    W("v", l_nx)
+    k_n16 = inc(v.tensor_copy(T["nxt16"][:], T["nxi"][:]))
+    inc(v.memset(tab[:, 4864:7168], float(NONE)), k_fill)
+    W("v", l_ow)
+    k_o16 = inc(v.tensor_copy(T["own16"][:], T["owi"][:]))
+    W("v", k_f0, k_f1, k_f2, k_fill, k_fd, k_vp, k_o16)
+    k_tab = inc(v.tensor_copy(tab[:, 0:8192].indirect(T["own16"][:, 0:128]), T["vr"][:]))
+    W("s", k_vp)
+    k_zx = inc(s.activation(T["xw"][:, 16:2064], T["vr"][:], AF.Copy, scale=0.0))
+
+    A, B = helpers(T, topo, core)
+    sent = 0
+    W("g", k_n16)
+    sent += write(g, T, topo, core, A, T["rln"][:], T["nxt16"][:], "rn", 8, 16)
+    W("g", k_z)
+    kb = inc(g.affine_select(T["basef"][:], T["zz"][:, 0:144], [[-512, 9], [1, 16]], OP.not_equal, 256.0, -15, 32))
+    W("g", k_p0)
+    sent += writes(g, T, topo, core, [(T.cores[(q - 4) % N], T["pt4"][:], T["pt0"][:], "ap4", 0, 4),
+                                      (T.cores[(q - 2) % N], T["pt2"][:], T["pt0"][:], "ap2", 4, 8)])
+    sent += write(g, T, topo, core, B, T["rlp"][:], T["pt0"][:], "rp", 8, 16)
+    W("g", kb)
+    k_bf = inc(g.affine_select(T["basef"][:], T["basef"][:], [[-512, 9], [1, 16]], OP.not_equal, 1.0, -271, 32))
+    k_c = tok()
+    for name in ("xw", "w5", "wd", "wb"):
+        inc(g.iota(T[name][:, 0:16], [[0, 16]], NONE, 0, **small), k_c)
+    k_b = inc(g.affine_select(T["base0"][:], T["zz"][:, 0:144], [[-512, 9], [1, 16]], OP.not_equal, 1.0, -143, 32))
+    k_on = inc(g.iota(T["on"][:], [[0, 160]], 1, 0, **small))
+    W("g", k_on)
+    k1 = inc(g.affine_select(T["bases"][:], T["on"][:, 0:144], [[0, 9], [1, 16]], OP.is_equal, 0.0, -15, 0))
+    k_ids = inc(g.affine_select(T["ids"][:], T["zz"][:, 0:128], [[1, 128]], OP.not_equal, 1.0, 0, -1))
+    W("g", k1)
+    k1 = inc(g.affine_select(T["bases"][:], T["bases"][:], [[-16, 9], [0, 16]], OP.is_ge, 0.0, -3, 1))
+    W("g", k1)
+    inc(g.affine_select(T["bases"][:], T["bases"][:], [[16, 9], [0, 16]], OP.is_ge, 0.0, 7, -1), k_b)
+
+    def gather2(outb, win, lst):
+        ks = []
+        for h in range(2):
+            k = tok()
+            a = 1024 * h
+            inc(v.tensor_copy(outb[:, a:a + 512], win.indirect(lst[:, a // 16:a // 16 + 32])), k)
+            inc(s.activation(outb[:, a + 512:a + 1024], win.indirect(lst[:, a // 16 + 32:a // 16 + 64]), AF.Copy), k)
+            ks.append(k)
+        return ks
+
+    R("v", "anx", 8)
+    R("s", "anx", 8)
+    W("v", k_tab)
+    W("s", k_tab)
+    kg = gather2(T["gr"], tab[:, 0:8192], T["nx"])
+
+    W("y", *kg)
+    k_xp = inc(g.sync.dma_start(T["xp"][:], T["gr"][4:128:16, :]), None, 16)
+    W("s", *kg)
+    k_xs = inc(g.scalar.dma_start(T["xs"][:], T["gr"][0:128:8, :]), None, 16)
+
+    pws = (T["pwa"], T["pwb"])
+    pqs = (T["px"], T["py"])
+
+    def wrap(pw, base, row, h, first=True, last=True):
+        for p in range(16):
+            op = t.matmul(pw[h][:, 0:64], T[base][:, 15 - p:143 - p], T[row][:, 1024 * h + p:1024 * h + 1024:16],
+                          first and p == 0, last and p == 15)
+        return op
+
+    def lists(out, h, kws, k):
+        W("v", kws[h])
+        inc(v.tensor_scalar(T[out][:, 64 * h:64 * h + 64], pqs[h][:, 0:64], 16.0, 0.0, OP.add, OP.max), k)
+
+    W("t", k_bf)
+    kw = []
+    for h in range(2):
+        W("t", kg[h])
+        kw.append(inc(wrap(pqs, "basef", "gr", h)))
+
+    k_f, k_z5 = tok(), tok()
+    inc(v.memset(T["w5"][:, 16:1040], 0.0), k_z5)
+    lists("f0", 0, kw, k_f)
+    inc(v.memset(T["w5"][:, 1040:2064], 0.0), k_z5)
+    lists("f0", 1, kw, k_f)
+    k_z2 = inc(s.activation(T["pr2"][:], T["vr"][:], AF.Copy, scale=0.0))
+
+    W("g", k_xs)
+    sent += write(g, T, topo, core, T.cores[(q - 2) % N], T["xr"][:], T["xs"][:], "ax")
+    W("g", k_f, k_xp)
+    sent += writes(g, T, topo, core, [(A, T["rlf"][:], T["f0"][:], "rf", 8, 16),
+                                      (B, T["rlq"][:], T["xp"][:], "rq", 4, 8),
+                                      (T.cores[(q - 4) % N], T["f4"][:], T["f0"][:], "af4", 0, 4)])
+
+    W("y", k_zx)
+    R("y", "ap1", 8)
+    k_xw = inc(g.sync.dma_start(T["xw"][3:128:16, 16:2064], T["pt1"][:]), None, 16)
+    W("y", k_z5)
+    R("y", "ap4", 4)
+    k_w5 = inc(g.sync.dma_start(T["w5"][6:128:16, 16:2064], T["pt4"][:]), None, 16)
+    W("y", k_z2)
+    R("y", "ap2", 4)
+    k_r2 = inc(g.sync.dma_start(T["pr2"][4:128:16, :], T["pt2"][:]), None, 16)
+    R("y", "ax", 8)
+    inc(g.sync.dma_start(T["xw"][0:128:8, 16:2064], T["xr"][:]), k_xw, 16)
+    R("y", "aq5", 8)
+    inc(g.sync.dma_start(T["w5"][7:128:16, 16:2064], T["pq5"][:]), k_w5, 16)
+    R("y", "aq3", 8)
+    inc(g.sync.dma_start(T["pr2"][5:128:16, :], T["pq3"][:]), k_r2, 16)
+
+    W("t", k_b, k_vp)
+    for h in range(2):
+        wrap(pws, "base0", "vr", h, True, False)
+
+    k3 = inc(v.tensor_scalar(T["pg"][:], T["ip"][:, 0:1], 4, 1, OP.arith_shift_right, OP.bitwise_and))
+    W("v", k3)
+    k2 = inc(v.tensor_copy(T["gf"][:], T["pg"][:]))
+    inc(v.tensor_scalar(T["ngf"][:], T["pg"][:], -1.0, 1.0, OP.mult, OP.add), k2)
+    W("v", k2, k_on)
+    k_nm = inc(v.tensor_scalar(T["msk"][:, 0:16], T["on"][:, 0:16], T["ngf"][:, 0:1], None, OP.mult))
+    inc(v.tensor_scalar(T["msk"][:, 16:32], T["on"][:, 0:16], T["gf"][:, 0:1], None, OP.mult), k_nm)
+    k3 = inc(v.tensor_scalar(T["loi"][:], T["owi"][:], 255, None, OP.bitwise_and))
+    W("v", k3)
+    inc(v.tensor_scalar(T["nlo"][:, 0:128], T["loi"][:], 1.0, None, OP.add), k_nm)
+    inc(v.tensor_tensor(T["nhi"][:, 0:128], T["owi"][:], T["loi"][:], OP.subtract), k_nm)
+
+    k_e = tok()
+    for name, a in (("sumw", 128), ("posk", 128), ("nlo", 128), ("nhi", 128), ("sc1", 0)):
+        inc(g.iota(T[name][:, a:a + 16], [[0, 16]], 0, 0, **small), k_e)
+    k1 = inc(g.affine_select(T["bo"][:], T["on"][:, 0:128], [[-16, 8], [0, 16]], OP.is_ge, 0.0, 0, 1))
+    k_kc = inc(g.iota(T["kc"][:], [[0, 8], [1, 16]], 0, 0, **small))
+    W("g", k1)
+    k_bo = inc(g.affine_select(T["bo"][:], T["bo"][:], [[16, 8], [0, 16]], OP.is_ge, 0.0, 15, -1))
+    inc(g.iota(T["m1"][:], [[1, 256]], 1, 0, **small), k_kc)
+    W("g", k_bo)
+    inc(g.affine_select(T["tri"][:], T["bo"][:], [[1, 128]], OP.is_ge, 0.0, 0, -1), k_e)
+
+    w5, wd, wb = T["w5"], T["wd"], T["wb"]
+    for x in "vs":
+        R(x, "af1", 8)
+        W(x, k_c, k_xw)
+    kx = gather2(T["xg"], T["xw"][:], T["f1"])
+    W("t", k_f)
+    kq, k_fg = [], tok()
+    for h in range(2):
+        W("t", kx[h])
+        kq.append(inc(wrap(pqs, "basef", "xg", h)))
+    for x in "vs":
+        R(x, "af4", 4)
+        W(x, k_w5)
+    k_d2 = inc(v.tensor_copy(wd[:, 16:1040], w5[:].indirect(T["f4"][:, 0:64])))
+    inc(s.activation(wd[:, 1040:2064], w5[:].indirect(T["f4"][:, 64:128]), AF.Copy), k_d2)
+    for h in range(2):
+        lists("fg", h, kq, k_fg)
+    SH = 1600
+    X = 2048 - SH
+    psa = T["psa"]
+    for x in "vs":
+        R(x, "af3", 8)
+        W(x, k_d2)
+    W("v", k_r2)
+    k_d3 = inc(v.tensor_tensor(wb[:, 16:16 + SH], wd[:].indirect(T["f3"][:, 0:SH // 16]), T["pr2"][:, 0:SH], OP.add))
+    ks = inc(s.activation(T["d3"][:, 0:X], wd[:].indirect(T["f3"][:, SH // 16:128]), AF.Copy))
+    W("t", k_ids, k_r2)
+    t.matmul(psa[:, 0:X], T["ids"][:], T["pr2"][:, SH:2048], True, False)
+    wrap(pws, "bases", "xg", 0, False, False)
+    W("t", ks)
+    kp = inc(t.matmul(psa[:, 0:X], T["ids"][:], T["d3"][:, 0:X], False, True))
+    wrap(pws, "bases", "xg", 1, False, False)
+    W("s", k_kc, k_bo)
+    k_sc = inc(s.activation(T["cp"][:], T["kc"][:], AF.Copy, scale=-1.0 / 2048))
+    inc(s.activation(T["ck"][:], T["kc"][:], AF.Copy, scale=-1.0 / 128), k_sc)
+    inc(s.activation(T["bo16"][:], T["bo"][:], AF.Copy, scale=1.0 / 16), k_sc)
+    inc(s.activation(T["half"][:], T["on"][:, 0:32], AF.Copy, scale=0.5), k_sc)
+    W("s", kp)
+    inc(s.activation(wb[:, 16 + SH:2064], psa[:, 0:X], AF.Copy), k_d3)
+
+    T1, T2, T3, CM = psa[:, 0:128], psa[:, 512:640], psa[:, 1024:1152], psa[:, 1536:1568]
+    W("t", k_sc, k_on)
+    t.matmul(T3, T["on"][:, 0:128], T["ck"][:], True, False)
+    t.matmul(T2, T["on"][:, 0:128], T["cp"][:], True, False)
+
+    W("v", k_d3, k_fg)
+    W("s", k_d3, k_fg)
+    kr = gather2(T["rr"], wb[:], T["fg"])
+    kw = []
+    for h in range(2):
+        W("t", kr[h])
+        kw.append(inc(wrap(pws, "bases", "rr", h, False, True)))
+
+    kt, sc1 = T["kt"], T["sc1"]
+    kk_ = []
+    for h in range(2):
+        W("v", kw[h])
+        kk_.append(inc(v.tensor_scalar(kt[:, 64 * h:64 * h + 64], pws[h][:, 0:64], 0.0, None, OP.is_ge)))
+    W("v", *kk_)
+    k_scan = inc(v.tensor_tensor_scan(sc1[:, 16:144], kt[:], kt[:], 0.0, OP.add, OP.max))
+    k_sum = tok()
+    for h in range(2):
+        W("s", kk_[h])
+        inc(s.activation(T["sumw"][:, 64 * h:64 * h + 64], pws[h][:, 0:64], AF.Copy), k_sum)
+    W("t", k_scan, k_e, k_fg, k_d3)
+    k_t1 = inc(t.matmul(T1, sc1[:, 16:144], T["bo16"][:], True, True))
+    k_t3 = inc(t.matmul(T3, sc1[:, 16:144], T["bo16"][:], False, True))
+    k_t2 = inc(t.matmul(T2, sc1[:, 16:144], T["bo16"][:], False, True))
+    t.matmul(T["px"][:, 0:128], T["bo"][:], sc1[:, 15:143], True, False)
+    k_pos = inc(t.matmul(T["px"][:, 0:128], T["tri"][:], kt[:], False, True))
+    W("v", k_t1)
+    k_a = inc(v.tensor_scalar(T["ai"][:], T1, -0.46875, None, OP.add))
+    W("s", k_t3)
+    k_sg = inc(s.activation(T["sg"][:], T3, AF.Sign, bias=-0.03125, scale=-1.0))
+    W("v", k_a, k_t2)
+    k_ab = inc(v.tensor_tensor(T["a1"][:], T2, T["ai"][:], OP.is_le))
+    W("v", k_kc)
+    inc(v.tensor_tensor(T["bb"][:], T["ai"][:], T["kc"][:], OP.is_equal), k_ab)
+    W("t", k_sg, k_ab)
+    for a in range(4):
+        c = slice(32 * a, 32 * a + 32)
+        t.matmul(psa[c, 1536:1568], T["half"][:], T["sg"][:, c], True, False)
+        op = t.matmul(psa[c, 1536:1568], T["a1"][:, c], T["bb"][:, c], False, True)
+        k_cm = inc(op, None if a == 0 else k_cm)
+    W("v", k_pos)
+    k_pk = inc(v.tensor_tensor(T["posk"][:, 0:128], T["px"][:, 0:128], kt[:], OP.mult))
+    W("v", k_bo)
+    k_bh = inc(v.tensor_copy(T["boh"][:], T["bo"][:, 0:128:16]))
+    W("v", k_cm, k_nm)
+    k1 = inc(v.tensor_tensor(T["cmm"][:], CM, T["msk"][:], OP.mult))
+    W("v", k1)
+    k2 = inc(v.tensor_tensor(T["lf"][:], T["cmm"][:, 0:16], T["cmm"][:, 16:32], OP.add))
+    W("v", k2)
+    k3 = inc(v.tensor_scalar(T["lst"][:], T["lf"][:], 64.0, None, OP.add))
+    W("v", k3, k_pk, k_e)
+    k_oh = inc(v.tensor_tensor(T["oh"][:], T["posk"][:].indirect(T["lst"][:]), T["m1"][:], OP.is_equal))
+    W("v", k_oh, k_sum)
+    k_vs = inc(v.tensor_tensor(T["vs"][:], T["sumw"][:].indirect(T["lst"][:]), T["oh"][:], OP.mult))
+    k_vh = inc(v.tensor_tensor(T["vh"][:], T["nhi"][:].indirect(T["lst"][:]), T["oh"][:], OP.mult))
+    k_vl = inc(v.tensor_tensor(T["vl"][:], T["nlo"][:].indirect(T["lst"][:]), T["oh"][:], OP.mult))
+    W("t", k_vs, k_bh)
+    k_ys = inc(t.matmul(T["px"][0:8, 0:256], T["boh"][:], T["vs"][:], True, True))
+    W("t", k_vh)
+    t.matmul(T["py"][0:8, 0:256], T["bo"][:, 0:128:16], T["vh"][:], True, False)
+    W("t", k_vl)
+    k_yk = inc(t.matmul(T["py"][0:8, 0:256], T["bo"][:, 0:128:16], T["vl"][:], False, True))
+    W("s", k_ys)
+    k1 = inc(s.activation(T["yss"][0:8, :], T["px"][0:8, 0:256], AF.Copy))
+    W("s", k1)
+    o1 = inc(g.scalar.dma_start(T.ys[:], T["yss"][0:8, :]), None, 16)
+    W("v", k_yk)
+    k2 = inc(v.tensor_scalar(T["yks"][0:8, :], T["py"][0:8, 0:256], -1.0, None, OP.add))
+    W("y", k2)
+    o2 = inc(g.sync.dma_start(T.yk[:], T["yks"][0:8, :]), None, 16)
+    W("s", o1)
+    W("y", o2)
+    g.wait_ge(T.sem["lc"], sent)

@@ -1,50 +1,41 @@
 from concourse.bass import DstId, RemoteDMATransfer
 from concourse.mybir import AluOpType as OP, ActivationFunctionType as AF
 
+
+def _sb(n, dt="bfloat16"):
+    return ("sbuf", [128, n], dt)
+
+
 SCRATCH = {
-    "nx": ("sbuf", [128, 128], "uint16"),
-    "rln": ("sbuf", [128, 128], "uint16"), "rlf": ("sbuf", [128, 128], "uint16"), "rlp": ("sbuf", [128, 128], "bfloat16"),
-    "rlq": ("dram", [128, 128], "bfloat16"),
-    "owi": ("sbuf", [128, 128], "int32"), "nxi": ("sbuf", [128, 128], "int32"), "pti": ("sbuf", [128, 128], "int32"),
-    "own16": ("sbuf", [128, 128], "uint16"), "nxt16": ("sbuf", [128, 128], "uint16"), "pt0": ("sbuf", [128, 128], "bfloat16"),
-    "tab": ("sbuf", [128, 8192], "bfloat16"), "vr": ("sbuf", [128, 2048], "bfloat16"), "gr": ("sbuf", [128, 2048], "bfloat16"),
-    "f0": ("sbuf", [128, 128], "uint16"), "fg": ("sbuf", [128, 128], "uint16"),
-    "xs": ("dram", [128, 256], "bfloat16"), "xr": ("dram", [128, 256], "bfloat16"),
-    "xp": ("dram", [128, 128], "bfloat16"), "pq5": ("dram", [128, 128], "bfloat16"), "pq3": ("dram", [128, 128], "bfloat16"),
-    "xw": ("sbuf", [128, 2064], "bfloat16"), "xg": ("sbuf", [128, 2048], "bfloat16"),
-    "w5": ("sbuf", [128, 2064], "bfloat16"), "wd": ("sbuf", [128, 2064], "bfloat16"), "wb": ("sbuf", [128, 2064], "bfloat16"),
-    "d3": ("sbuf", [128, 512], "bfloat16"), "rr": ("sbuf", [128, 2048], "bfloat16"), "pr2": ("sbuf", [128, 2048], "bfloat16"),
-    "lo": ("sbuf", [128, 256], "bfloat16"), "m1": ("sbuf", [128, 256], "bfloat16"), "ip": ("sbuf", [128, 2], "int32"),
-    "io8": ("sbuf", [128, 8], "float32"), "pb": ("sbuf", [128, 1], "int32"),
-    "pg": ("sbuf", [128, 1], "int32"),
-    "ml": ("sbuf", [128, 1], "float32"), "nml": ("sbuf", [128, 1], "float32"), "hb": ("sbuf", [128, 8], "float32"),
-    "gf": ("sbuf", [128, 1], "float32"), "ngf": ("sbuf", [128, 1], "float32"),
-    "zz": ("sbuf", [128, 160], "bfloat16"), "on": ("sbuf", [128, 160], "bfloat16"), "half": ("sbuf", [128, 32], "bfloat16"),
-    "basef": ("sbuf", [128, 144], "bfloat16"), "bases": ("sbuf", [128, 144], "bfloat16"), "base0": ("sbuf", [128, 144], "bfloat16"),
-    "ids": ("sbuf", [128, 128], "bfloat16"),
-    "bo": ("sbuf", [128, 128], "bfloat16"), "tri": ("sbuf", [128, 128], "bfloat16"), "bo16": ("sbuf", [128, 128], "bfloat16"),
-    "boh": ("sbuf", [128, 8], "float16"), "kc": ("sbuf", [128, 128], "bfloat16"), "cp": ("sbuf", [128, 128], "bfloat16"),
-    "ck": ("sbuf", [128, 128], "bfloat16"), "msk": ("sbuf", [128, 32], "float32"),
-    "loi": ("sbuf", [128, 128], "int32"), "nlo": ("sbuf", [128, 144], "bfloat16"), "nhi": ("sbuf", [128, 144], "bfloat16"),
-    "kt": ("sbuf", [128, 128], "bfloat16"), "sc1": ("sbuf", [128, 144], "bfloat16"), "sumw": ("sbuf", [128, 144], "float32"),
-    "posk": ("sbuf", [128, 144], "bfloat16"), "ai": ("sbuf", [128, 128], "int32"), "a1": ("sbuf", [128, 128], "bfloat16"),
-    "bb": ("sbuf", [128, 128], "bfloat16"), "sg": ("sbuf", [128, 128], "bfloat16"), "cmm": ("sbuf", [128, 32], "float32"),
-    "lf": ("sbuf", [128, 16], "float32"), "lst": ("sbuf", [128, 16], "uint16"), "oh": ("sbuf", [128, 256], "bfloat16"),
-    "vs": ("sbuf", [128, 256], "float16"), "vh": ("sbuf", [128, 256], "bfloat16"), "vl": ("sbuf", [128, 256], "bfloat16"),
-    "yks": ("sbuf", [128, 256], "float32"), "yss": ("sbuf", [128, 256], "float32"),
+    "rln": _sb(128, "uint16"), "rlf": _sb(128, "uint16"), "rlt": _sb(128), "rlq": ("dram", [128, 128], "bfloat16"),
+    "owi": _sb(128, "int32"), "nxi": _sb(128, "int32"), "pti": _sb(128, "int32"),
+    "own16": _sb(128, "uint16"), "nxt16": _sb(128, "uint16"), "pt0": _sb(128), "nx": _sb(128, "uint16"), "pt4": _sb(128),
+    "tab": _sb(8192), "vr": _sb(2064), "gr": _sb(2064), "xg": _sb(2048), "wd": _sb(2064), "rr": _sb(2048),
+    "f0": _sb(128, "uint16"), "f3": _sb(128, "uint16"), "fa": _sb(128, "uint16"),
+    "fb0": _sb(64, "uint16"), "fb1": _sb(64, "uint16"), "fa0": _sb(64, "uint16"), "fa1": _sb(64, "uint16"),
+    "as": _sb(128), "at": _sb(128), "xsum": _sb(128, "float32"), "xt": _sb(128, "float32"),
+    "xs": ("dram", [256, 128], "bfloat16"), "xr": ("dram", [256, 128], "bfloat16"),
+    "xp": ("dram", [128, 128], "bfloat16"), "pq5": ("dram", [128, 128], "bfloat16"),
+    "lo": _sb(256), "m1": _sb(256), "ip": _sb(2, "int32"), "io8": _sb(8, "float32"), "pb": _sb(1, "int32"),
+    "ml": _sb(1, "float32"), "nml": _sb(1, "float32"), "hb": _sb(8, "float32"), "pf": _sb(1, "float32"),
+    "gi": _sb(1, "int32"), "gp": _sb(1, "float32"), "pg": _sb(1, "int32"), "gq": _sb(1, "float32"),
+    "zz": _sb(144), "on": _sb(128), "half": _sb(32), "basef": _sb(144), "bases": _sb(144), "base0": _sb(144),
+    "ids": _sb(128), "jg": _sb(128), "bo": _sb(128), "tri": _sb(128), "bo16": _sb(128),
+    "kc": _sb(128), "cp": _sb(128), "ck": _sb(128), "c47": _sb(128), "msk": _sb(32, "float32"),
+    "of": _sb(36, "float32"), "oh16": _sb(36, "float16"), "nam": _sb(144, "float32"),
+    "kt": _sb(128), "sc1": _sb(144), "sumw": _sb(144, "float32"), "posk": _sb(144),
+    "aa": _sb(128), "nfl": _sb(128), "ee": _sb(128), "sg": _sb(128), "cmm": _sb(32, "float32"),
+    "lf": _sb(16, "float32"), "lst": _sb(16, "uint16"), "oh": _sb(256), "vs": _sb(256, "float16"), "vn": _sb(256, "float32"),
+    "yks": _sb(64, "float32"), "yss": _sb(64, "float32"),
     "psa": ("psum", [128, 2048], "float32"), "pwa": ("psum", [128, 512], "float32"), "pwb": ("psum", [128, 512], "float32"),
     "px": ("psum", [128, 512], "float32"), "py": ("psum", [128, 512], "float32"),
 }
-for _k in (1, 3, 4):
-    SCRATCH["f%d" % _k] = ("sbuf", [128, 128], "uint16")
-for _k in (1, 2, 4):
-    SCRATCH["pt%d" % _k] = ("sbuf", [128, 128], "bfloat16")
 NTOK = 130
-SEMAPHORES = (["t%d" % _k for _k in range(NTOK)] + ["anx", "rn", "rf", "rp", "rq", "lc", "ax", "af1", "af3", "af4", "aq3", "aq5"]
-              + ["ap1", "ap2", "ap4"])
+SEMAPHORES = ["t%d" % _k for _k in range(NTOK)] + ["anx", "rn", "rf", "rq", "rt", "lc", "ax", "af", "aq", "at", "ap", "ag0", "ag1", "as"]
 
-ODD = (5, 3, 1)
 NONE = -2048
+ROUND = 12582912.0
+FILL_V, FILL_D = 3328, 1024
 
 
 def engs(topo, src, dst, a, b):
@@ -70,34 +61,23 @@ def writes(g, T, topo, src, parts):
     return n
 
 
-def helpers(T, topo, rc):
+HANDED = (("rn", "rln", 1, "nx", "anx"), ("rf", "rlf", -3, "f3", "af"), ("rq", "rlq", -5, "pq5", "aq"), ("rt", "rlt", -1, "at", "at"))
+
+
+def helper(T, topo, rc):
     q, N = T.rank_of(rc), len(T.cores)
-    far = [T.cores[(q + 1) % N]] + [T.cores[(q - k) % N] for k in ODD]
-    c = [x for x in topo.cores_of(rc) if x != rc and topo.die(x) == topo.die(rc) and all(topo.may_write(x, d) for d in far)]
-    return c[0], c[1]
+    far = [T.cores[(q + h[2]) % N] for h in HANDED]
+    return [x for x in topo.cores_of(rc) if x != rc and topo.die(x) == topo.die(rc) and all(topo.may_write(x, d) for d in far)][0]
 
 
 def hand_on(g, core, T, topo):
     N = len(T.cores)
     for rc in T.cores:
-        if rc not in topo.cores_of(core):
-            continue
-        q = T.rank_of(rc)
-        A, B = helpers(T, topo, rc)
-        sent = 0
-        if core == A:
-            g.wait_ge(T.sem["rn"], 8)
-            sent += write(g, T, topo, core, T.cores[(q + 1) % N], T["nx"][:], T["rln"][:], "anx")
-            g.wait_ge(T.sem["rf"], 8)
-            sent += write(g, T, topo, core, T.cores[(q - 1) % N], T["f1"][:], T["rlf"][:], "af1")
-            sent += write(g, T, topo, core, T.cores[(q - 3) % N], T["f3"][:], T["rlf"][:], "af3")
-        elif core == B:
-            g.wait_ge(T.sem["rp"], 8)
-            sent += write(g, T, topo, core, T.cores[(q - 1) % N], T["pt1"][:], T["rlp"][:], "ap1")
-            g.wait_ge(T.sem["rq"], 4)
-            sent += write(g, T, topo, core, T.cores[(q - 5) % N], T["pq5"][:], T["rlq"][:], "aq5")
-            sent += write(g, T, topo, core, T.cores[(q - 3) % N], T["pq3"][:], T["rlq"][:], "aq3")
-        if sent:
+        if rc in topo.cores_of(core) and core == helper(T, topo, rc):
+            q, sent = T.rank_of(rc), 0
+            for here, buf, d, out, there in HANDED:
+                g.wait_ge(T.sem[here], 8)
+                sent += write(g, T, topo, core, T.cores[(q + d) % N], T[out][:], T[buf][:], there)
             g.wait_ge(T.sem["lc"], sent)
 
 
@@ -128,33 +108,30 @@ def rank_program(g, core, T, topo):
                 seen[(queue, k[2])] = k[1]
                 Q[queue].wait_ge(k[0], k[1])
 
-    def R(queue, sem, n):
-        if (queue, sem) not in seen:
-            seen[(queue, sem)] = n
-            Q[queue].wait_ge(T.sem[sem], n)
+    def R(queues, sem, n=8):
+        for x in queues:
+            Q[x].wait_ge(T.sem[sem], n)
 
-    l_ow = inc(g.sync.dma_start(T["owi"][:], T.own[:]), None, 16)
-    l_nx = inc(g.scalar.dma_start(T["nxi"][:], T.nxt[:]), None, 16)
+    def ring(d):
+        return T.cores[(q + d) % N]
+
+    tab, vr, gr, wd, psa = T["tab"], T["vr"], T["gr"], T["wd"], T["psa"]
+
     l_pt = inc(g.sync.dma_start(T["pti"][:], T.pts[:]), None, 16)
+    l_nx = inc(g.scalar.dma_start(T["nxi"][:], T.nxt[:]), None, 16)
+    l_ow = inc(g.sync.dma_start(T["owi"][:], T.own[:]), None, 16)
 
-    tab = T["tab"]
     k_i = inc(g.iota(T["ip"][:, 0:1], [[0, 1]], 0, 1))
     inc(g.iota(T["io8"][:], [[1, 8]], 0, 0, **small), k_i)
     k_lo = inc(g.iota(T["lo"][:], [[1, 256]], 0, 0, **small))
-    k_fill = inc(g.iota(tab[:, 7168:8192], [[0, 1024]], NONE, 0, **small))
-
+    a_d, a_v = 8192 - FILL_V - FILL_D, 8192 - FILL_V
     k_f0 = inc(v.memset(tab[:, 0:512], float(NONE)))
     k_f1 = inc(v.memset(tab[:, 512:1024], float(NONE)))
     W("y", k_f0, k_f1)
-    k_fd = inc(g.sync.dma_start(tab[:, 3840:4864], tab[:, 0:1024]), None, 16)
+    k_fd = inc(g.sync.dma_start(tab[:, a_d:a_v], tab[:, 0:FILL_D]), None, 16)
     W("s", k_f0)
     k_f2 = inc(s.activation(tab[:, 1024:1536], tab[:, 0:512], AF.Copy))
-    W("s", k_f1)
-    inc(s.activation(tab[:, 1536:2560], tab[:, 0:1024], AF.Copy), k_fill)
-    W("s", k_f2)
-    inc(s.activation(tab[:, 2560:3840], tab[:, 0:1280], AF.Copy), k_fill)
 
-    k_z = inc(v.memset(T["zz"][:], 0.0))
     W("v", k_i)
     k1 = inc(v.tensor_scalar(T["pb"][:], T["ip"][:, 0:1], 3, 1, OP.arith_shift_right, OP.bitwise_and))
     W("v", k1)
@@ -162,260 +139,243 @@ def rank_program(g, core, T, topo):
     k3 = inc(v.tensor_scalar(T["nml"][:], T["pb"][:], -1.0, 1.0, OP.mult, OP.add))
     W("v", k3)
     inc(v.tensor_scalar(T["hb"][:], T["io8"][:], T["nml"][:, 0:1], None, OP.mult), k2)
+    k_fill = inc(v.memset(tab[:, a_v:a_v + 256], float(NONE)))
     W("v", k2, k_lo)
+    W("s", k2, k_lo)
     k_vr = tok()
     for b in range(8):
-        inc(v.tensor_scalar(T["vr"][:, 256 * b:256 * b + 256], T["lo"][:], T["ml"][:, 0:1], T["hb"][:, b:b + 1], OP.mult, OP.add), k_vr)
+        out = vr[:, 16 + 256 * b:272 + 256 * b]
+        if b < 6:
+            inc(v.tensor_scalar(out, T["lo"][:], T["ml"][:, 0:1], T["hb"][:, b:b + 1], OP.mult, OP.add), k_vr)
+        else:
+            inc(s.activation(out, T["lo"][:], AF.Identity, bias=T["hb"][:, b:b + 1], scale=T["ml"][:, 0:1]), k_vr)
+    W("s", k_f1, k_f2)
+    a = 1536
+    while a < a_d:
+        n = min(1536, a_d - a)
+        inc(s.activation(tab[:, a:a + n], tab[:, 0:n], AF.Copy), k_fill)
+        a += n
+    inc(v.memset(tab[:, a_v + 256:a_v + 768], float(NONE)), k_fill)
     W("v", l_pt)
     k_p0 = inc(v.tensor_copy(T["pt0"][:], T["pti"][:]))
     W("y", k_vr, k_p0)
-    k_vp = inc(g.sync.dma_start(T["vr"][4:128:16, :], T["pt0"][:]), None, 16)
+    k_vp = inc(g.sync.dma_start(vr[4:128:16, 16:2064], T["pt0"][:]), None, 16)
     W("v", l_nx)
     k_n16 = inc(v.tensor_copy(T["nxt16"][:], T["nxi"][:]))
-    inc(v.memset(tab[:, 4864:7168], float(NONE)), k_fill)
+    inc(v.memset(tab[:, a_v + 768:8192], float(NONE)), k_fill)
     W("v", l_ow)
     k_o16 = inc(v.tensor_copy(T["own16"][:], T["owi"][:]))
     W("v", k_f0, k_f1, k_f2, k_fill, k_fd, k_vp, k_o16)
-    k_tab = inc(v.tensor_copy(tab[:, 0:8192].indirect(T["own16"][:, 0:128]), T["vr"][:]))
-    W("s", k_vp)
-    k_zx = inc(s.activation(T["xw"][:, 16:2064], T["vr"][:], AF.Copy, scale=0.0))
+    k_tab = inc(v.tensor_copy(tab[:, 0:8192].indirect(T["own16"][:, 0:128]), vr[:, 16:2064]))
 
-    A, B = helpers(T, topo, core)
-    sent = 0
-    W("g", k_n16)
-    sent += write(g, T, topo, core, A, T["rln"][:], T["nxt16"][:], "rn", 8, 16)
+    H = helper(T, topo, core)
+    k_z = inc(g.iota(T["zz"][:], [[0, 144]], 0, 0, **small))
     W("g", k_z)
-    kb = inc(g.affine_select(T["basef"][:], T["zz"][:, 0:144], [[-512, 9], [1, 16]], OP.not_equal, 256.0, -15, 32))
-    W("g", k_p0)
-    sent += writes(g, T, topo, core, [(T.cores[(q - 4) % N], T["pt4"][:], T["pt0"][:], "ap4", 0, 4),
-                                      (T.cores[(q - 2) % N], T["pt2"][:], T["pt0"][:], "ap2", 4, 8)])
-    sent += write(g, T, topo, core, B, T["rlp"][:], T["pt0"][:], "rp", 8, 16)
+    kb = inc(g.affine_select(T["basef"][:], T["zz"][:], [[-512, 9], [1, 16]], OP.not_equal, 256.0, -15, 32))
+    W("g", k_n16)
+    sent = write(g, T, topo, core, H, T["rln"][:], T["nxt16"][:], "rn", 8, 16)
     W("g", kb)
     k_bf = inc(g.affine_select(T["basef"][:], T["basef"][:], [[-512, 9], [1, 16]], OP.not_equal, 1.0, -271, 32))
-    k_c = tok()
-    for name in ("xw", "w5", "wd", "wb"):
-        inc(g.iota(T[name][:, 0:16], [[0, 16]], NONE, 0, **small), k_c)
-    k_b = inc(g.affine_select(T["base0"][:], T["zz"][:, 0:144], [[-512, 9], [1, 16]], OP.not_equal, 1.0, -143, 32))
-    k_on = inc(g.iota(T["on"][:], [[0, 160]], 1, 0, **small))
-    W("g", k_on)
-    k1 = inc(g.affine_select(T["bases"][:], T["on"][:, 0:144], [[0, 9], [1, 16]], OP.is_equal, 0.0, -15, 0))
-    k_ids = inc(g.affine_select(T["ids"][:], T["zz"][:, 0:128], [[1, 128]], OP.not_equal, 1.0, 0, -1))
-    W("g", k1)
-    k1 = inc(g.affine_select(T["bases"][:], T["bases"][:], [[-16, 9], [0, 16]], OP.is_ge, 0.0, -3, 1))
-    W("g", k1)
-    inc(g.affine_select(T["bases"][:], T["bases"][:], [[16, 9], [0, 16]], OP.is_ge, 0.0, 7, -1), k_b)
-
-    def gather2(outb, win, lst):
-        ks = []
-        for h in range(2):
-            k = tok()
-            a = 1024 * h
-            inc(v.tensor_copy(outb[:, a:a + 512], win.indirect(lst[:, a // 16:a // 16 + 32])), k)
-            inc(s.activation(outb[:, a + 512:a + 1024], win.indirect(lst[:, a // 16 + 32:a // 16 + 64]), AF.Copy), k)
-            ks.append(k)
-        return ks
-
-    R("v", "anx", 8)
-    R("s", "anx", 8)
-    W("v", k_tab)
-    W("s", k_tab)
-    kg = gather2(T["gr"], tab[:, 0:8192], T["nx"])
-
-    W("y", *kg)
-    k_xp = inc(g.sync.dma_start(T["xp"][:], T["gr"][4:128:16, :]), None, 16)
-    W("s", *kg)
-    k_xs = inc(g.scalar.dma_start(T["xs"][:], T["gr"][0:128:8, :]), None, 16)
+    k_b0 = inc(g.affine_select(T["base0"][:], T["zz"][:], [[-512, 9], [1, 16]], OP.not_equal, 1.0, -143, 32))
+    W("g", k_p0)
+    sent += write(g, T, topo, core, ring(-4), T["pt4"][:], T["pt0"][:], "ap")
+    k_j = inc(g.iota(T["jg"][:], [[1, 8], [0, 16]], 0, 0, **small))
+    inc(g.iota(T["kc"][:], [[0, 8], [1, 16]], 0, 0, **small), k_j)
 
     pws = (T["pwa"], T["pwb"])
     pqs = (T["px"], T["py"])
 
-    def wrap(pw, base, row, h, first=True, last=True):
+    def wrap(out, base, row, a, n=1024, first=True, last=True):
         for p in range(16):
-            op = t.matmul(pw[h][:, 0:64], T[base][:, 15 - p:143 - p], T[row][:, 1024 * h + p:1024 * h + 1024:16],
-                          first and p == 0, last and p == 15)
+            op = t.matmul(out, T[base][:, 15 - p:143 - p], row[:, a + p:a + n:16], first and p == 0, last and p == 15)
         return op
 
-    def lists(out, h, kws, k):
+    def lists(out, h, kws):
         W("v", kws[h])
-        inc(v.tensor_scalar(T[out][:, 64 * h:64 * h + 64], pqs[h][:, 0:64], 16.0, 0.0, OP.add, OP.max), k)
+        return v.tensor_scalar(out, pqs[h][:, 0:64], 16.0, 0.0, OP.add, OP.max)
 
+    def gather(out, a, win, lst, c, nv=512, k=None):
+        k = inc(v.tensor_copy(out[:, a:a + nv], win.indirect(lst[:, c:c + nv // 16])), k)
+        return inc(s.activation(out[:, a + nv:a + 1024], win.indirect(lst[:, c + nv // 16:c + 64]), AF.Copy), k)
+
+    W("t", k_b0, k_vp)
+    for h in range(2):
+        k_pw = inc(wrap(pws[h][:, 0:64], "base0", vr, 16 + 1024 * h, 1024, True, False), None if h == 0 else k_pw)
+
+    R("vs", "anx")
+    W("v", k_tab)
+    W("s", k_tab)
+    kg = [gather(gr, 16 + 1024 * h, tab[:, 0:8192], T["nx"], 64 * h) for h in range(2)]
+    W("s", *kg)
+    k_xs = inc(g.scalar.dma_start(T["xs"][:], gr[0:128:8, 16:2064]), None, 16)
+    W("y", *kg)
+    inc(g.sync.dma_start(T["xp"][:], gr[4:128:16, 16:2064]), k_xs, 16)
     W("t", k_bf)
     kw = []
     for h in range(2):
         W("t", kg[h])
-        kw.append(inc(wrap(pqs, "basef", "gr", h)))
+        kw.append(inc(wrap(pqs[h][:, 0:64], "basef", gr, 16 + 1024 * h)))
+    k_aw = inc(wrap(psa[:, 0:128], "base0", gr, 16, 2048))
 
-    k_f, k_z5 = tok(), tok()
-    inc(v.memset(T["w5"][:, 16:1040], 0.0), k_z5)
-    lists("f0", 0, kw, k_f)
-    inc(v.memset(T["w5"][:, 1040:2064], 0.0), k_z5)
-    lists("f0", 1, kw, k_f)
-    k_z2 = inc(s.activation(T["pr2"][:], T["vr"][:], AF.Copy, scale=0.0))
+    k_f = inc(lists(T["f0"][:, 0:64], 0, kw))
+    k1 = inc(v.tensor_scalar(T["gi"][:], T["ip"][:, 0:1], 4, None, OP.arith_shift_right))
+    inc(v.tensor_scalar(T["pg"][:], T["ip"][:, 0:1], 4, 1, OP.arith_shift_right, OP.bitwise_and), k1)
+    inc(v.tensor_copy(T["pf"][:], T["ip"][:, 0:1]), k1)
+    inc(v.memset(T["on"][:], 1.0), k1)
+    inc(lists(T["f0"][:, 64:128], 1, kw), k_f)
 
+    W("g", k_f)
+    sent += write(g, T, topo, core, H, T["rlf"][:], T["f0"][:], "rf", 8, 16)
     W("g", k_xs)
-    sent += write(g, T, topo, core, T.cores[(q - 2) % N], T["xr"][:], T["xs"][:], "ax")
-    W("g", k_f, k_xp)
-    sent += writes(g, T, topo, core, [(A, T["rlf"][:], T["f0"][:], "rf", 8, 16),
-                                      (B, T["rlq"][:], T["xp"][:], "rq", 4, 8),
-                                      (T.cores[(q - 4) % N], T["f4"][:], T["f0"][:], "af4", 0, 4)])
+    sent += writes(g, T, topo, core, [(ring(-4), T["xr"][0:128, :], T["xs"][0:128, :], "ax", 0, 4),
+                                      (ring(-4), T["xr"][128:256, :], T["xs"][128:256, :], "ax", 4, 8),
+                                      (H, T["rlq"][:], T["xp"][:], "rq", 8, 16)])
 
-    W("y", k_zx)
-    R("y", "ap1", 8)
-    k_xw = inc(g.sync.dma_start(T["xw"][3:128:16, 16:2064], T["pt1"][:]), None, 16)
-    W("y", k_z5)
-    R("y", "ap4", 4)
-    k_w5 = inc(g.sync.dma_start(T["w5"][6:128:16, 16:2064], T["pt4"][:]), None, 16)
-    W("y", k_z2)
-    R("y", "ap2", 4)
-    k_r2 = inc(g.sync.dma_start(T["pr2"][4:128:16, :], T["pt2"][:]), None, 16)
-    R("y", "ax", 8)
-    inc(g.sync.dma_start(T["xw"][0:128:8, 16:2064], T["xr"][:]), k_xw, 16)
-    R("y", "aq5", 8)
-    inc(g.sync.dma_start(T["w5"][7:128:16, 16:2064], T["pq5"][:]), k_w5, 16)
-    R("y", "aq3", 8)
-    inc(g.sync.dma_start(T["pr2"][5:128:16, :], T["pq3"][:]), k_r2, 16)
+    k_c = tok()
+    for name, a, val in (("gr", 0, NONE), ("vr", 0, NONE), ("wd", 0, NONE), ("sumw", 128, 0), ("posk", 128, 0), ("nam", 128, 0), ("sc1", 0, 0)):
+        inc(s.activation(T[name][:, a:a + 16], T["lo"][:, 0:16], AF.Identity, bias=float(val), scale=0.0), k_c)
+    W("s", k_pw)
+    R("s", "ap")
+    k_w = inc(g.scalar.dma_start(vr[0:128:16, 16:2064], T["pt4"][:]), None, 16)
+    W("s", k_aw)
+    k_as = inc(s.activation(T["as"][:], psa[:, 0:128], AF.Copy))
+    W("g", k_as)
+    sent += write(g, T, topo, core, H, T["rlt"][:], T["as"][:], "rt", 8, 16)
 
-    W("t", k_b, k_vp)
-    for h in range(2):
-        wrap(pws, "base0", "vr", h, True, False)
+    W("y", k_xs, k_aw, k_pw)
+    R("y", "ax")
+    k_xw = inc(g.sync.dma_start(gr[0:128:8, 16:2064], T["xr"][:]), None, 16)
+    R("y", "aq")
+    inc(g.sync.dma_start(vr[8:128:16, 16:2064], T["pq5"][:]), k_w, 16)
 
-    k3 = inc(v.tensor_scalar(T["pg"][:], T["ip"][:, 0:1], 4, 1, OP.arith_shift_right, OP.bitwise_and))
+    W("v", k1, k_j)
+    k2 = inc(v.tensor_copy(T["gp"][:], T["gi"][:]))
+    inc(v.tensor_scalar(T["gq"][:], T["gi"][:], 4.0, 3.0, OP.mult, OP.add), k2)
+    k_k = inc(v.tensor_scalar(T["bases"][:], T["basef"][:], 0.0, None, OP.is_gt))
+    inc(v.tensor_scalar(T["ids"][:], T["lo"][:, 0:128], T["pf"][:, 0:1], None, OP.is_equal), k_k)
+    k3 = inc(v.tensor_copy(T["ml"][:], T["pg"][:]))
+    W("v", k2)
+    k_bo = inc(v.tensor_scalar(T["bo"][:], T["jg"][:], T["gp"][:, 0:1], None, OP.is_equal))
+    inc(v.tensor_scalar(T["of"][:], T["lo"][:, 0:36], T["gq"][:, 0:1], None, OP.is_equal), k_k)
+    inc(v.tensor_scalar(T["oh16"][:], T["lo"][:, 0:36], T["gq"][:, 0:1], None, OP.is_equal), k_k)
     W("v", k3)
-    k2 = inc(v.tensor_copy(T["gf"][:], T["pg"][:]))
-    inc(v.tensor_scalar(T["ngf"][:], T["pg"][:], -1.0, 1.0, OP.mult, OP.add), k2)
-    W("v", k2, k_on)
-    k_nm = inc(v.tensor_scalar(T["msk"][:, 0:16], T["on"][:, 0:16], T["ngf"][:, 0:1], None, OP.mult))
-    inc(v.tensor_scalar(T["msk"][:, 16:32], T["on"][:, 0:16], T["gf"][:, 0:1], None, OP.mult), k_nm)
-    k3 = inc(v.tensor_scalar(T["loi"][:], T["owi"][:], 255, None, OP.bitwise_and))
-    W("v", k3)
-    inc(v.tensor_scalar(T["nlo"][:, 0:128], T["loi"][:], 1.0, None, OP.add), k_nm)
-    inc(v.tensor_tensor(T["nhi"][:, 0:128], T["owi"][:], T["loi"][:], OP.subtract), k_nm)
-
-    k_e = tok()
-    for name, a in (("sumw", 128), ("posk", 128), ("nlo", 128), ("nhi", 128), ("sc1", 0)):
-        inc(g.iota(T[name][:, a:a + 16], [[0, 16]], 0, 0, **small), k_e)
-    k1 = inc(g.affine_select(T["bo"][:], T["on"][:, 0:128], [[-16, 8], [0, 16]], OP.is_ge, 0.0, 0, 1))
-    k_kc = inc(g.iota(T["kc"][:], [[0, 8], [1, 16]], 0, 0, **small))
-    W("g", k1)
-    k_bo = inc(g.affine_select(T["bo"][:], T["bo"][:], [[16, 8], [0, 16]], OP.is_ge, 0.0, 15, -1))
-    inc(g.iota(T["m1"][:], [[1, 256]], 1, 0, **small), k_kc)
+    k_m = inc(v.tensor_scalar(T["msk"][:], T["jg"][:, 0:32], T["ml"][:, 0:1], None, OP.is_equal))
+    inc(v.tensor_scalar(T["m1"][:], T["lo"][:], 1.0, None, OP.add), k_m)
+    inc(v.tensor_scalar(T["nam"][:, 0:128], T["owi"][:], 1.0, None, OP.add), k_m)
     W("g", k_bo)
-    inc(g.affine_select(T["tri"][:], T["bo"][:], [[1, 128]], OP.is_ge, 0.0, 0, -1), k_e)
-
-    w5, wd, wb = T["w5"], T["wd"], T["wb"]
-    for x in "vs":
-        R(x, "af1", 8)
-        W(x, k_c, k_xw)
-    kx = gather2(T["xg"], T["xw"][:], T["f1"])
-    W("t", k_f)
-    kq, k_fg = [], tok()
-    for h in range(2):
-        W("t", kx[h])
-        kq.append(inc(wrap(pqs, "basef", "xg", h)))
-    for x in "vs":
-        R(x, "af4", 4)
-        W(x, k_w5)
-    k_d2 = inc(v.tensor_copy(wd[:, 16:1040], w5[:].indirect(T["f4"][:, 0:64])))
-    inc(s.activation(wd[:, 1040:2064], w5[:].indirect(T["f4"][:, 64:128]), AF.Copy), k_d2)
-    for h in range(2):
-        lists("fg", h, kq, k_fg)
-    SH = 1600
-    X = 2048 - SH
-    psa = T["psa"]
-    for x in "vs":
-        R(x, "af3", 8)
-        W(x, k_d2)
-    W("v", k_r2)
-    k_d3 = inc(v.tensor_tensor(wb[:, 16:16 + SH], wd[:].indirect(T["f3"][:, 0:SH // 16]), T["pr2"][:, 0:SH], OP.add))
-    ks = inc(s.activation(T["d3"][:, 0:X], wd[:].indirect(T["f3"][:, SH // 16:128]), AF.Copy))
-    W("t", k_ids, k_r2)
-    t.matmul(psa[:, 0:X], T["ids"][:], T["pr2"][:, SH:2048], True, False)
-    wrap(pws, "bases", "xg", 0, False, False)
-    W("t", ks)
-    kp = inc(t.matmul(psa[:, 0:X], T["ids"][:], T["d3"][:, 0:X], False, True))
-    wrap(pws, "bases", "xg", 1, False, False)
-    W("s", k_kc, k_bo)
-    k_sc = inc(s.activation(T["cp"][:], T["kc"][:], AF.Copy, scale=-1.0 / 2048))
+    inc(g.affine_select(T["tri"][:], T["bo"][:], [[1, 128]], OP.is_ge, 0.0, 0, -1), k_k)
+    W("s", k1, k_j, k_bo)
+    k_sc = inc(s.activation(T["cp"][:], T["kc"][:], AF.Identity, scale=-2.0 / 4096, bias=-17.0 / 4096))
     inc(s.activation(T["ck"][:], T["kc"][:], AF.Copy, scale=-1.0 / 128), k_sc)
+    inc(s.activation(T["c47"][:], T["on"][:], AF.Copy, scale=-15.0 / 4096), k_sc)
     inc(s.activation(T["bo16"][:], T["bo"][:], AF.Copy, scale=1.0 / 16), k_sc)
     inc(s.activation(T["half"][:], T["on"][:, 0:32], AF.Copy, scale=0.5), k_sc)
-    W("s", kp)
-    inc(s.activation(wb[:, 16 + SH:2064], psa[:, 0:X], AF.Copy), k_d3)
+    T1, T2, T3, T4, CM = psa[:, 0:128], psa[:, 512:640], psa[:, 1024:1152], psa[:, 1536:1664], T["py"][:, 0:32]
+    W("t", k_sc)
+    t.matmul(T2, T["on"][:], T["cp"][:], True, False)
+    t.matmul(T3, T["on"][:], T["ck"][:], True, False)
+    t.matmul(T4, T["on"][:], T["ck"][:], True, False)
+    t.matmul(T4, T["on"][:], T["c47"][:], False, False)
 
-    T1, T2, T3, CM = psa[:, 0:128], psa[:, 512:640], psa[:, 1024:1152], psa[:, 1536:1568]
-    W("t", k_sc, k_on)
-    t.matmul(T3, T["on"][:, 0:128], T["ck"][:], True, False)
-    t.matmul(T2, T["on"][:, 0:128], T["cp"][:], True, False)
-
-    W("v", k_d3, k_fg)
-    W("s", k_d3, k_fg)
-    kr = gather2(T["rr"], wb[:], T["fg"])
+    R("vs", "af")
+    W("v", k_c, k_xw)
+    W("s", k_c, k_xw)
+    kx = [gather(T["xg"], 1024 * h, gr[:], T["f3"], 64 * h) for h in range(2)]
+    W("t", k_f)
+    kq = []
+    for h in range(2):
+        W("t", kx[h])
+        kq.append(inc(wrap(pqs[h][:, 0:64], "basef", T["xg"], 1024 * h)))
+    W("v", k_w)
+    W("s", k_w)
+    kd = []
+    for h in range(2):
+        fa = T["fa%d" % h]
+        k = inc(lists(fa[:], h, kq))
+        W("g", k)
+        sent += write(g, T, topo, core, ring(2), T["fb%d" % h][:], fa[:], "ag%d" % h)
+        W("v", k)
+        W("s", k)
+        kd.append(gather(wd, 16 + 1024 * h, vr[:], fa, 0, 480))
+    W("t", k_k, k_as)
+    for h in range(2):
+        W("t", kd[h])
+        k_x = inc(wrap(psa[:, 64 * h:64 * h + 64], "bases", wd, 16 + 1024 * h), None if h == 0 else k_x)
+    W("v", *kd)
+    W("s", *kd)
+    R("t", "at")
     kw = []
     for h in range(2):
-        W("t", kr[h])
-        kw.append(inc(wrap(pws, "bases", "rr", h, False, True)))
+        R("vs", "ag%d" % h)
+        kr = gather(T["rr"], 1024 * h, wd[:], T["fb%d" % h], 0, 544)
+        if h == 0:
+            W("s", k_x)
+            k_xu = inc(s.activation(T["xsum"][:], psa[:, 0:128], AF.Copy))
+            W("g", k_xu)
+            sent += write(g, T, topo, core, ring(2), T["xt"][:], T["xsum"][:], "as")
+        t.matmul(pws[h][:, 0:64], T["ids"][:], T["at"][:, 64 * h:64 * h + 64], False, False)
+        W("t", kr)
+        kw.append(inc(wrap(pws[h][:, 0:64], "bases", T["rr"], 1024 * h, 1024, False, True)))
 
     kt, sc1 = T["kt"], T["sc1"]
-    kk_ = []
+    k_kt = tok()
     for h in range(2):
         W("v", kw[h])
-        kk_.append(inc(v.tensor_scalar(kt[:, 64 * h:64 * h + 64], pws[h][:, 0:64], 0.0, None, OP.is_ge)))
-    W("v", *kk_)
+        inc(v.tensor_scalar(kt[:, 64 * h:64 * h + 64], pws[h][:, 0:64], 0.0, None, OP.is_ge), k_kt)
+    W("v", k_kt)
     k_scan = inc(v.tensor_tensor_scan(sc1[:, 16:144], kt[:], kt[:], 0.0, OP.add, OP.max))
-    k_sum = tok()
-    for h in range(2):
-        W("s", kk_[h])
-        inc(s.activation(T["sumw"][:, 64 * h:64 * h + 64], pws[h][:, 0:64], AF.Copy), k_sum)
-    W("t", k_scan, k_e, k_fg, k_d3)
-    k_t1 = inc(t.matmul(T1, sc1[:, 16:144], T["bo16"][:], True, True))
-    k_t3 = inc(t.matmul(T3, sc1[:, 16:144], T["bo16"][:], False, True))
-    k_t2 = inc(t.matmul(T2, sc1[:, 16:144], T["bo16"][:], False, True))
+    W("t", k_scan, k_c, k_xu)
+    k4 = inc(t.matmul(T4, sc1[:, 16:144], T["bo16"][:], False, True))
+    k3 = inc(t.matmul(T3, sc1[:, 16:144], T["bo16"][:], False, True))
+    k2 = inc(t.matmul(T2, sc1[:, 16:144], T["bo16"][:], False, True))
+    k1 = inc(t.matmul(T1, sc1[:, 16:144], T["bo16"][:], True, True))
     t.matmul(T["px"][:, 0:128], T["bo"][:], sc1[:, 15:143], True, False)
     k_pos = inc(t.matmul(T["px"][:, 0:128], T["tri"][:], kt[:], False, True))
-    W("v", k_t1)
-    k_a = inc(v.tensor_scalar(T["ai"][:], T1, -0.46875, None, OP.add))
-    W("s", k_t3)
-    k_sg = inc(s.activation(T["sg"][:], T3, AF.Sign, bias=-0.03125, scale=-1.0))
-    W("v", k_a, k_t2)
-    k_ab = inc(v.tensor_tensor(T["a1"][:], T2, T["ai"][:], OP.is_le))
-    W("v", k_kc)
-    inc(v.tensor_tensor(T["bb"][:], T["ai"][:], T["kc"][:], OP.is_equal), k_ab)
-    W("t", k_sg, k_ab)
+    W("v", k4)
+    k_ab = inc(v.tensor_scalar(T["ee"][:], T4, ROUND, ROUND, OP.add, OP.is_equal))
+    W("s", k3)
+    inc(s.activation(T["sg"][:], T3, AF.Sign, bias=-0.03125, scale=-1.0), k_ab)
+    W("v", k2)
+    inc(v.tensor_scalar(T["nfl"][:], T2, -1.0, -192.0, OP.mult, OP.add), k_ab)
+    W("s", k1)
+    inc(s.activation(T["aa"][:], T1, AF.Identity, bias=192.0 - 0.46875), k_ab)
+    W("t", k_ab)
     for a in range(4):
         c = slice(32 * a, 32 * a + 32)
-        t.matmul(psa[c, 1536:1568], T["half"][:], T["sg"][:, c], True, False)
-        op = t.matmul(psa[c, 1536:1568], T["a1"][:, c], T["bb"][:, c], False, True)
-        k_cm = inc(op, None if a == 0 else k_cm)
+        t.matmul(T["py"][c, 0:32], T["half"][:], T["sg"][:, c], True, False)
+        t.matmul(T["py"][c, 0:32], T["aa"][:, c], T["ee"][:, c], False, False)
+        op = t.matmul(T["py"][c, 0:32], T["nfl"][:, c], T["ee"][:, c], False, True)
+    k_cm = inc(op)
     W("v", k_pos)
     k_pk = inc(v.tensor_tensor(T["posk"][:, 0:128], T["px"][:, 0:128], kt[:], OP.mult))
-    W("v", k_bo)
-    k_bh = inc(v.tensor_copy(T["boh"][:], T["bo"][:, 0:128:16]))
-    W("v", k_cm, k_nm)
+    R("v", "as")
+    for h in range(2):
+        inc(v.tensor_tensor(T["sumw"][:, 64 * h:64 * h + 64], pws[h][:, 0:64], T["xt"][:, 64 * h:64 * h + 64], OP.add), k_pk)
+    W("v", k_cm, k_m)
     k1 = inc(v.tensor_tensor(T["cmm"][:], CM, T["msk"][:], OP.mult))
     W("v", k1)
     k2 = inc(v.tensor_tensor(T["lf"][:], T["cmm"][:, 0:16], T["cmm"][:, 16:32], OP.add))
     W("v", k2)
     k3 = inc(v.tensor_scalar(T["lst"][:], T["lf"][:], 64.0, None, OP.add))
-    W("v", k3, k_pk, k_e)
+    W("v", k3, k_pk)
     k_oh = inc(v.tensor_tensor(T["oh"][:], T["posk"][:].indirect(T["lst"][:]), T["m1"][:], OP.is_equal))
-    W("v", k_oh, k_sum)
+    W("v", k_oh)
+    k_vn = inc(v.tensor_tensor(T["vn"][:], T["nam"][:].indirect(T["lst"][:]), T["oh"][:], OP.mult))
     k_vs = inc(v.tensor_tensor(T["vs"][:], T["sumw"][:].indirect(T["lst"][:]), T["oh"][:], OP.mult))
-    k_vh = inc(v.tensor_tensor(T["vh"][:], T["nhi"][:].indirect(T["lst"][:]), T["oh"][:], OP.mult))
-    k_vl = inc(v.tensor_tensor(T["vl"][:], T["nlo"][:].indirect(T["lst"][:]), T["oh"][:], OP.mult))
-    W("t", k_vs, k_bh)
-    k_ys = inc(t.matmul(T["px"][0:8, 0:256], T["boh"][:], T["vs"][:], True, True))
-    W("t", k_vh)
-    t.matmul(T["py"][0:8, 0:256], T["bo"][:, 0:128:16], T["vh"][:], True, False)
-    W("t", k_vl)
-    k_yk = inc(t.matmul(T["py"][0:8, 0:256], T["bo"][:, 0:128:16], T["vl"][:], False, True))
-    W("s", k_ys)
-    k1 = inc(s.activation(T["yss"][0:8, :], T["px"][0:8, 0:256], AF.Copy))
+    ky = []
+    for out, sel, val, k in (("py", "of", "vn", k_vn), ("px", "oh16", "vs", k_vs)):
+        W("t", k)
+        for a in range(4):
+            op = t.matmul(T[out][0:32, 0:64], T[sel][:, 3 - a:35 - a], T[val][:, 64 * a:64 * a + 64], a == 0, a == 3)
+        ky.append(inc(op))
+    W("s", ky[0])
+    k1 = inc(s.activation(T["yks"][0:32, :], T["py"][0:32, 0:64], AF.Identity, bias=-1.0))
     W("s", k1)
-    o1 = inc(g.scalar.dma_start(T.ys[:], T["yss"][0:8, :]), None, 16)
-    W("v", k_yk)
-    k2 = inc(v.tensor_scalar(T["yks"][0:8, :], T["py"][0:8, 0:256], -1.0, None, OP.add))
+    o1 = inc(g.scalar.dma_start(T.yk[:], T["yks"][0:32, :]), None, 16)
+    W("v", ky[1])
+    k2 = inc(v.tensor_copy(T["yss"][0:32, :], T["px"][0:32, 0:64]))
     W("y", k2)
-    o2 = inc(g.sync.dma_start(T.yk[:], T["yks"][0:8, :]), None, 16)
+    o2 = inc(g.sync.dma_start(T.ys[:], T["yss"][0:32, :]), None, 16)
     W("s", o1)
     W("y", o2)
     g.wait_ge(T.sem["lc"], sent)

@@ -11,31 +11,29 @@ SCRATCH = {
     "owi": _sb(128, "int32"), "nxi": _sb(128, "int32"), "pti": _sb(128, "int32"),
     "own16": _sb(128, "uint16"), "nxt16": _sb(128, "uint16"), "pt0": _sb(128), "nx": _sb(128, "uint16"), "pt4": _sb(128),
     "tab": _sb(8192), "vr": _sb(2064), "gr": _sb(2064), "xg": _sb(2048), "wd": _sb(2064), "rr": _sb(2048),
-    "f0": _sb(128, "uint16"), "f3": _sb(128, "uint16"), "fa": _sb(128, "uint16"),
-    "fb0": _sb(64, "uint16"), "fb1": _sb(64, "uint16"), "fa0": _sb(64, "uint16"), "fa1": _sb(64, "uint16"),
-    "as": _sb(128), "at": _sb(128), "xsum": _sb(128, "float32"), "xt": _sb(128, "float32"),
-    "xs": ("dram", [256, 128], "bfloat16"), "xr": ("dram", [256, 128], "bfloat16"),
-    "xp": ("dram", [128, 128], "bfloat16"), "pq5": ("dram", [128, 128], "bfloat16"),
-    "lo": _sb(256), "m1": _sb(256), "ip": _sb(2, "int32"), "io8": _sb(8, "float32"), "pb": _sb(1, "int32"),
-    "ml": _sb(1, "float32"), "nml": _sb(1, "float32"), "hb": _sb(8, "float32"), "pf": _sb(1, "float32"),
-    "gi": _sb(1, "int32"), "gp": _sb(1, "float32"), "pg": _sb(1, "int32"), "gq": _sb(1, "float32"),
+    "f": _sb(128, "uint16"), "fi": _sb(128, "uint16"), "fa": _sb(128, "uint16"), "fb": _sb(128, "uint16"), "fc": _sb(128, "uint16"),
+    "as": _sb(128), "at": _sb(128), "xsum": _sb(128, "float16"), "xt": _sb(128, "float16"),
+    "xp": ("dram", [128, 128], "bfloat16"), "pq": ("dram", [128, 128], "bfloat16"),
+    "lo": _sb(256), "m1": _sb(256), "hi": _sb(256), "ip": _sb(1, "int32"), "pf": _sb(1, "float32"), "gb": _sb(1),
+    "off": _sb(1, "float32"), "gi": _sb(1, "int32"), "gp": _sb(1, "float32"), "gq": _sb(1, "float32"),
     "zz": _sb(144), "on": _sb(128), "half": _sb(32), "basef": _sb(144), "bases": _sb(144), "base0": _sb(144),
-    "ids": _sb(128), "jg": _sb(128), "bo": _sb(128), "tri": _sb(128), "bo16": _sb(128),
-    "kc": _sb(128), "cp": _sb(128), "ck": _sb(128), "c47": _sb(128), "msk": _sb(32, "float32"),
+    "ids": _sb(128), "id16": _sb(128, "float16"), "id32": _sb(128, "float32"), "jg": _sb(128), "bo": _sb(128), "tri": _sb(128),
+    "bo16": _sb(128), "kc": _sb(128), "cp": _sb(128), "ck": _sb(128), "c47": _sb(128),
     "of": _sb(36, "float32"), "oh16": _sb(36, "float16"), "nam": _sb(144, "float32"),
-    "kt": _sb(128), "sc1": _sb(144), "sumw": _sb(144, "float32"), "posk": _sb(144),
-    "aa": _sb(128), "nfl": _sb(128), "ee": _sb(128), "sg": _sb(128), "cmm": _sb(32, "float32"),
-    "lf": _sb(16, "float32"), "lst": _sb(16, "uint16"), "oh": _sb(256), "vs": _sb(256, "float16"), "vn": _sb(256, "float32"),
+    "kt": _sb(128), "sc1": _sb(144), "sum0": _sb(128, "float32"), "sumw": _sb(144, "float32"), "posk": _sb(144),
+    "aa": _sb(128), "nfl": _sb(128), "ee": _sb(128), "sg": _sb(128),
+    "lst": _sb(16, "uint16"), "oh": _sb(256), "vs": _sb(256, "float16"), "vn": _sb(256, "float32"),
     "yks": _sb(64, "float32"), "yss": _sb(64, "float32"),
     "psa": ("psum", [128, 2048], "float32"), "pwa": ("psum", [128, 512], "float32"), "pwb": ("psum", [128, 512], "float32"),
     "px": ("psum", [128, 512], "float32"), "py": ("psum", [128, 512], "float32"),
 }
-NTOK = 130
-SEMAPHORES = ["t%d" % _k for _k in range(NTOK)] + ["anx", "rn", "rf", "rq", "rt", "lc", "ax", "af", "aq", "at", "ap", "ag0", "ag1", "as"]
+NTOK = 128
+SEMAPHORES = ["t%d" % _k for _k in range(NTOK)] + ["anx", "rn", "rf0", "rf1", "rq", "rt", "lc", "af0", "af1", "aq", "at", "ap",
+                                                   "ab", "ac0", "ac1", "as"]
 
 NONE = -2048
 ROUND = 12582912.0
-FILL_V, FILL_D = 3328, 1024
+FILL_V, FILL_D, FILL_G = 3328, 1024, 320
 
 
 def engs(topo, src, dst, a, b):
@@ -50,23 +48,13 @@ def write(g, T, topo, src, dst, out, in_, sem, a=0, b=8):
     return k
 
 
-def writes(g, T, topo, src, parts):
-    tr, n = [], 0
-    for dst, out, in_, sem, a, b in parts:
-        rid, pid = topo.addr(dst, src)
-        m, k = engs(topo, src, dst, a, b)
-        n += k
-        tr.append(RemoteDMATransfer(dst_ids=[DstId(rid=rid, pnc=pid)], dma_engine_mask=m, remote_sem=T.sem[sem], src=in_, dst=out))
-    g.remote_dma_fused(tr, local_sem=T.sem["lc"])
-    return n
-
-
-HANDED = (("rn", "rln", 1, "nx", "anx"), ("rf", "rlf", -3, "f3", "af"), ("rq", "rlq", -5, "pq5", "aq"), ("rt", "rlt", -1, "at", "at"))
+HANDED = (("rn", 8, "rln", 0, 128, 1, "nx", "anx"), ("rf0", 16, "rlf", 0, 64, 1, "fi", "af0"), ("rf1", 16, "rlf", 64, 128, 1, "fi", "af1"),
+          ("rq", 8, "rlq", 0, 128, -5, "pq", "aq"), ("rt", 8, "rlt", 0, 128, -1, "at", "at"))
 
 
 def helper(T, topo, rc):
     q, N = T.rank_of(rc), len(T.cores)
-    far = [T.cores[(q + h[2]) % N] for h in HANDED]
+    far = [T.cores[(q + h[5]) % N] for h in HANDED]
     return [x for x in topo.cores_of(rc) if x != rc and topo.die(x) == topo.die(rc) and all(topo.may_write(x, d) for d in far)][0]
 
 
@@ -75,9 +63,9 @@ def hand_on(g, core, T, topo):
     for rc in T.cores:
         if rc in topo.cores_of(core) and core == helper(T, topo, rc):
             q, sent = T.rank_of(rc), 0
-            for here, buf, d, out, there in HANDED:
-                g.wait_ge(T.sem[here], 8)
-                sent += write(g, T, topo, core, T.cores[(q + d) % N], T[out][:], T[buf][:], there)
+            for here, n, buf, a, b, d, out, there in HANDED:
+                g.wait_ge(T.sem[here], n)
+                sent += write(g, T, topo, core, T.cores[(q + d) % N], T[out][:, a:b], T[buf][:, a:b], there)
             g.wait_ge(T.sem["lc"], sent)
 
 
@@ -118,72 +106,69 @@ def rank_program(g, core, T, topo):
     tab, vr, gr, wd, psa = T["tab"], T["vr"], T["gr"], T["wd"], T["psa"]
 
     l_pt = inc(g.sync.dma_start(T["pti"][:], T.pts[:]), None, 16)
-    l_nx = inc(g.scalar.dma_start(T["nxi"][:], T.nxt[:]), None, 16)
+    l_nx = inc(g.sync.dma_start(T["nxi"][:], T.nxt[:]), None, 16)
     l_ow = inc(g.sync.dma_start(T["owi"][:], T.own[:]), None, 16)
 
-    k_i = inc(g.iota(T["ip"][:, 0:1], [[0, 1]], 0, 1))
-    inc(g.iota(T["io8"][:], [[1, 8]], 0, 0, **small), k_i)
-    k_lo = inc(g.iota(T["lo"][:], [[1, 256]], 0, 0, **small))
-    a_d, a_v = 8192 - FILL_V - FILL_D, 8192 - FILL_V
+    k_lo = inc(g.iota(vr[:, 16:272], [[0, 2], [1, 128]], 0, 0, **small))
+    k_hi = inc(g.iota(T["hi"][0:64, :], [[1, 2], [0, 128]], 0, 2, **small))
+    a_g = 8192 - FILL_G
+    a_d, a_v = a_g - FILL_V - FILL_D, a_g - FILL_V
+    k_fg = inc(g.iota(tab[:, a_g:8192], [[0, FILL_G]], NONE, 0, **small))
     k_f0 = inc(v.memset(tab[:, 0:512], float(NONE)))
     k_f1 = inc(v.memset(tab[:, 512:1024], float(NONE)))
     W("y", k_f0, k_f1)
     k_fd = inc(g.sync.dma_start(tab[:, a_d:a_v], tab[:, 0:FILL_D]), None, 16)
     W("s", k_f0)
     k_f2 = inc(s.activation(tab[:, 1024:1536], tab[:, 0:512], AF.Copy))
-
-    W("v", k_i)
-    k1 = inc(v.tensor_scalar(T["pb"][:], T["ip"][:, 0:1], 3, 1, OP.arith_shift_right, OP.bitwise_and))
-    W("v", k1)
-    k2 = inc(v.tensor_copy(T["ml"][:], T["pb"][:]))
-    k3 = inc(v.tensor_scalar(T["nml"][:], T["pb"][:], -1.0, 1.0, OP.mult, OP.add))
-    W("v", k3)
-    inc(v.tensor_scalar(T["hb"][:], T["io8"][:], T["nml"][:, 0:1], None, OP.mult), k2)
-    k_fill = inc(v.memset(tab[:, a_v:a_v + 256], float(NONE)))
-    W("v", k2, k_lo)
-    W("s", k2, k_lo)
+    k_fill = inc(v.memset(tab[:, a_v:a_v + 512], float(NONE)))
+    W("v", k_lo)
+    W("s", k_lo)
     k_vr = tok()
-    for b in range(8):
+    for b in range(1, 8):
         out = vr[:, 16 + 256 * b:272 + 256 * b]
-        if b < 6:
-            inc(v.tensor_scalar(out, T["lo"][:], T["ml"][:, 0:1], T["hb"][:, b:b + 1], OP.mult, OP.add), k_vr)
-        else:
-            inc(s.activation(out, T["lo"][:], AF.Identity, bias=T["hb"][:, b:b + 1], scale=T["ml"][:, 0:1]), k_vr)
+        inc(v.tensor_copy(out, vr[:, 16:272]) if b <= 5 else s.activation(out, vr[:, 16:272], AF.Copy), k_vr)
+    W("y", k_vr, k_hi)
+    k_vp = inc(g.sync.dma_start(vr[0:128:16, 16:2064], T["hi"][0:64, :]), None, 16)
     W("s", k_f1, k_f2)
-    a = 1536
-    while a < a_d:
+    for a in range(1536, a_d, 1536):
         n = min(1536, a_d - a)
         inc(s.activation(tab[:, a:a + n], tab[:, 0:n], AF.Copy), k_fill)
-        a += n
-    inc(v.memset(tab[:, a_v + 256:a_v + 768], float(NONE)), k_fill)
+    inc(v.memset(tab[:, a_v + 512:a_v + 896], float(NONE)), k_fill)
     W("v", l_pt)
     k_p0 = inc(v.tensor_copy(T["pt0"][:], T["pti"][:]))
-    W("y", k_vr, k_p0)
-    k_vp = inc(g.sync.dma_start(vr[4:128:16, 16:2064], T["pt0"][:]), None, 16)
+    W("y", k_p0)
+    inc(g.sync.dma_start(vr[4:128:16, 16:2064], T["pt0"][:]), k_vp, 16)
     W("v", l_nx)
     k_n16 = inc(v.tensor_copy(T["nxt16"][:], T["nxi"][:]))
-    inc(v.memset(tab[:, a_v + 768:8192], float(NONE)), k_fill)
+    inc(v.memset(tab[:, a_v + 896:a_g], float(NONE)), k_fill)
     W("v", l_ow)
     k_o16 = inc(v.tensor_copy(T["own16"][:], T["owi"][:]))
-    W("v", k_f0, k_f1, k_f2, k_fill, k_fd, k_vp, k_o16)
+    W("v", k_f0, k_f1, k_f2, k_fill, k_fd, k_fg, k_vp, k_o16)
     k_tab = inc(v.tensor_copy(tab[:, 0:8192].indirect(T["own16"][:, 0:128]), vr[:, 16:2064]))
 
     H = helper(T, topo, core)
-    k_z = inc(g.iota(T["zz"][:], [[0, 144]], 0, 0, **small))
-    W("g", k_z)
-    kb = inc(g.affine_select(T["basef"][:], T["zz"][:], [[-512, 9], [1, 16]], OP.not_equal, 256.0, -15, 32))
     W("g", k_n16)
     sent = write(g, T, topo, core, H, T["rln"][:], T["nxt16"][:], "rn", 8, 16)
+    k_pf = inc(g.iota(T["pf"][:], [[0, 1]], 0, 1, **small))
+    k_z = inc(g.iota(T["zz"][:], [[0, 144]], 0, 0, **small))
+    W("g", k_z)
+    kb = inc(g.affine_select(T["basef"][:], T["zz"][:], [[-512, 9], [1, 16]], OP.not_equal, 128.0, -15, 32))
+    k_b0 = inc(g.affine_select(T["base0"][:], T["zz"][:], [[-512, 9], [1, 16]], OP.not_equal, 1.0, -143, 32))
     W("g", kb)
     k_bf = inc(g.affine_select(T["basef"][:], T["basef"][:], [[-512, 9], [1, 16]], OP.not_equal, 1.0, -271, 32))
-    k_b0 = inc(g.affine_select(T["base0"][:], T["zz"][:], [[-512, 9], [1, 16]], OP.not_equal, 1.0, -143, 32))
     W("g", k_p0)
     sent += write(g, T, topo, core, ring(-4), T["pt4"][:], T["pt0"][:], "ap")
-    k_j = inc(g.iota(T["jg"][:], [[1, 8], [0, 16]], 0, 0, **small))
+    k_lo = inc(g.iota(T["lo"][:], [[1, 256]], 0, 0, **small))
+    k_j = inc(g.iota(T["ip"][:], [[0, 1]], 0, 1))
+    inc(g.iota(T["jg"][:], [[1, 8], [0, 16]], 0, 0, **small), k_j)
     inc(g.iota(T["kc"][:], [[0, 8], [1, 16]], 0, 0, **small), k_j)
+    W("s", k_pf)
+    W("s", inc(s.activation(T["gb"][:], T["pf"][:], AF.Identity, scale=1.0 / 16, bias=192.0 - 0.46875)))
+    k_off = inc(s.activation(T["off"][:], T["gb"][:], AF.Identity, scale=-2048.0, bias=192.0 * 2048 + 16))
 
     pws = (T["pwa"], T["pwb"])
     pqs = (T["px"], T["py"])
+    halves = (slice(0, 64), slice(64, 128))
 
     def wrap(out, base, row, a, n=1024, first=True, last=True):
         for p in range(16):
@@ -192,45 +177,38 @@ def rank_program(g, core, T, topo):
 
     def lists(out, h, kws):
         W("v", kws[h])
-        return v.tensor_scalar(out, pqs[h][:, 0:64], 16.0, 0.0, OP.add, OP.max)
+        return inc(v.tensor_scalar(T[out][:, halves[h]], pqs[h][:, 0:64], T["off"][:, 0:1], 0.0, OP.add, OP.max))
 
-    def gather(out, a, win, lst, c, nv=512, k=None):
-        k = inc(v.tensor_copy(out[:, a:a + nv], win.indirect(lst[:, c:c + nv // 16])), k)
-        return inc(s.activation(out[:, a + nv:a + 1024], win.indirect(lst[:, c + nv // 16:c + 64]), AF.Copy), k)
+    def gather(out, a, win, lst, h, nv=512):
+        c = 64 * h
+        k = inc(v.tensor_copy(out[:, a:a + nv], win.indirect(T[lst][:, c:c + nv // 16])))
+        return inc(s.activation(out[:, a + nv:a + 1024], win.indirect(T[lst][:, c + nv // 16:c + 64]), AF.Copy), k)
 
     W("t", k_b0, k_vp)
     for h in range(2):
         k_pw = inc(wrap(pws[h][:, 0:64], "base0", vr, 16 + 1024 * h, 1024, True, False), None if h == 0 else k_pw)
 
     R("vs", "anx")
-    W("v", k_tab)
+    W("v", k_tab, k_off)
     W("s", k_tab)
-    kg = [gather(gr, 16 + 1024 * h, tab[:, 0:8192], T["nx"], 64 * h) for h in range(2)]
-    W("s", *kg)
-    k_xs = inc(g.scalar.dma_start(T["xs"][:], gr[0:128:8, 16:2064]), None, 16)
+    kg = [gather(gr, 16 + 1024 * h, tab[:, 0:8192], "nx", h) for h in range(2)]
     W("y", *kg)
-    inc(g.sync.dma_start(T["xp"][:], gr[4:128:16, 16:2064]), k_xs, 16)
+    k_xs = inc(g.sync.dma_start(T["xp"][:], gr[4:128:16, 16:2064]), None, 16)
     W("t", k_bf)
     kw = []
     for h in range(2):
         W("t", kg[h])
         kw.append(inc(wrap(pqs[h][:, 0:64], "basef", gr, 16 + 1024 * h)))
     k_aw = inc(wrap(psa[:, 0:128], "base0", gr, 16, 2048))
+    k_f = [lists("f", h, kw) for h in range(2)]
 
-    k_f = inc(lists(T["f0"][:, 0:64], 0, kw))
-    k1 = inc(v.tensor_scalar(T["gi"][:], T["ip"][:, 0:1], 4, None, OP.arith_shift_right))
-    inc(v.tensor_scalar(T["pg"][:], T["ip"][:, 0:1], 4, 1, OP.arith_shift_right, OP.bitwise_and), k1)
-    inc(v.tensor_copy(T["pf"][:], T["ip"][:, 0:1]), k1)
-    inc(v.memset(T["on"][:], 1.0), k1)
-    inc(lists(T["f0"][:, 64:128], 1, kw), k_f)
-
-    W("g", k_f)
-    sent += write(g, T, topo, core, H, T["rlf"][:], T["f0"][:], "rf", 8, 16)
+    for h in range(2):
+        W("g", k_f[h])
+        sent += write(g, T, topo, core, H, T["rlf"][:, halves[h]], T["f"][:, halves[h]], "rf%d" % h, 0, 16)
     W("g", k_xs)
-    sent += writes(g, T, topo, core, [(ring(-4), T["xr"][0:128, :], T["xs"][0:128, :], "ax", 0, 4),
-                                      (ring(-4), T["xr"][128:256, :], T["xs"][128:256, :], "ax", 4, 8),
-                                      (H, T["rlq"][:], T["xp"][:], "rq", 8, 16)])
+    sent += write(g, T, topo, core, H, T["rlq"][:], T["xp"][:], "rq", 8, 16)
 
+    W("s", k_lo)
     k_c = tok()
     for name, a, val in (("gr", 0, NONE), ("vr", 0, NONE), ("wd", 0, NONE), ("sumw", 128, 0), ("posk", 128, 0), ("nam", 128, 0), ("sc1", 0, 0)):
         inc(s.activation(T[name][:, a:a + 16], T["lo"][:, 0:16], AF.Identity, bias=float(val), scale=0.0), k_c)
@@ -241,88 +219,86 @@ def rank_program(g, core, T, topo):
     k_as = inc(s.activation(T["as"][:], psa[:, 0:128], AF.Copy))
     W("g", k_as)
     sent += write(g, T, topo, core, H, T["rlt"][:], T["as"][:], "rt", 8, 16)
-
-    W("y", k_xs, k_aw, k_pw)
-    R("y", "ax")
-    k_xw = inc(g.sync.dma_start(gr[0:128:8, 16:2064], T["xr"][:]), None, 16)
+    W("y", k_pw)
     R("y", "aq")
-    inc(g.sync.dma_start(vr[8:128:16, 16:2064], T["pq5"][:]), k_w, 16)
+    inc(g.sync.dma_start(vr[8:128:16, 16:2064], T["pq"][:]), k_w, 16)
 
-    W("v", k1, k_j)
+    W("v", k_j, k_lo, k_pf)
+    k1 = inc(v.tensor_scalar(T["gi"][:], T["ip"][:], 4, None, OP.arith_shift_right))
+    k_on = inc(v.memset(T["on"][:], 1.0))
+    k_k = inc(v.tensor_scalar(T["bases"][:], T["basef"][:], 0.0, None, OP.is_gt))
+    W("v", k1)
     k2 = inc(v.tensor_copy(T["gp"][:], T["gi"][:]))
     inc(v.tensor_scalar(T["gq"][:], T["gi"][:], 4.0, 3.0, OP.mult, OP.add), k2)
-    k_k = inc(v.tensor_scalar(T["bases"][:], T["basef"][:], 0.0, None, OP.is_gt))
-    inc(v.tensor_scalar(T["ids"][:], T["lo"][:, 0:128], T["pf"][:, 0:1], None, OP.is_equal), k_k)
-    k3 = inc(v.tensor_copy(T["ml"][:], T["pg"][:]))
+    for name in ("ids", "id16", "id32"):
+        inc(v.tensor_scalar(T[name][:], T["lo"][:, 0:128], T["pf"][:, 0:1], None, OP.is_equal), k_k)
     W("v", k2)
     k_bo = inc(v.tensor_scalar(T["bo"][:], T["jg"][:], T["gp"][:, 0:1], None, OP.is_equal))
-    inc(v.tensor_scalar(T["of"][:], T["lo"][:, 0:36], T["gq"][:, 0:1], None, OP.is_equal), k_k)
-    inc(v.tensor_scalar(T["oh16"][:], T["lo"][:, 0:36], T["gq"][:, 0:1], None, OP.is_equal), k_k)
-    W("v", k3)
-    k_m = inc(v.tensor_scalar(T["msk"][:], T["jg"][:, 0:32], T["ml"][:, 0:1], None, OP.is_equal))
-    inc(v.tensor_scalar(T["m1"][:], T["lo"][:], 1.0, None, OP.add), k_m)
+    for name in ("of", "oh16"):
+        inc(v.tensor_scalar(T[name][:], T["lo"][:, 0:36], T["gq"][:, 0:1], None, OP.is_equal), k_k)
+    k_m = inc(v.tensor_scalar(T["m1"][:], T["lo"][:], 1.0, None, OP.add))
     inc(v.tensor_scalar(T["nam"][:, 0:128], T["owi"][:], 1.0, None, OP.add), k_m)
     W("g", k_bo)
     inc(g.affine_select(T["tri"][:], T["bo"][:], [[1, 128]], OP.is_ge, 0.0, 0, -1), k_k)
-    W("s", k1, k_j, k_bo)
+    W("s", k_on, k_j, k_bo)
     k_sc = inc(s.activation(T["cp"][:], T["kc"][:], AF.Identity, scale=-2.0 / 4096, bias=-17.0 / 4096))
     inc(s.activation(T["ck"][:], T["kc"][:], AF.Copy, scale=-1.0 / 128), k_sc)
     inc(s.activation(T["c47"][:], T["on"][:], AF.Copy, scale=-15.0 / 4096), k_sc)
     inc(s.activation(T["bo16"][:], T["bo"][:], AF.Copy, scale=1.0 / 16), k_sc)
     inc(s.activation(T["half"][:], T["on"][:, 0:32], AF.Copy, scale=0.5), k_sc)
-    T1, T2, T3, T4, CM = psa[:, 0:128], psa[:, 512:640], psa[:, 1024:1152], psa[:, 1536:1664], T["py"][:, 0:32]
+    T1, T2, T3, T4, CM = psa[:, 0:128], psa[:, 512:640], psa[:, 1024:1152], psa[:, 1536:1664], T["py"][:, 0:16]
     W("t", k_sc)
     t.matmul(T2, T["on"][:], T["cp"][:], True, False)
     t.matmul(T3, T["on"][:], T["ck"][:], True, False)
     t.matmul(T4, T["on"][:], T["ck"][:], True, False)
     t.matmul(T4, T["on"][:], T["c47"][:], False, False)
 
-    R("vs", "af")
-    W("v", k_c, k_xw)
-    W("s", k_c, k_xw)
-    kx = [gather(T["xg"], 1024 * h, gr[:], T["f3"], 64 * h) for h in range(2)]
-    W("t", k_f)
+    W("v", k_c)
+    W("s", k_c)
+    W("t", *k_f)
     kq = []
     for h in range(2):
-        W("t", kx[h])
+        R("vs", "af%d" % h)
+        W("t", gather(T["xg"], 1024 * h, gr[:], "fi", h))
         kq.append(inc(wrap(pqs[h][:, 0:64], "basef", T["xg"], 1024 * h)))
+    for h in range(2):
+        W("g", lists("fa", h, kq))
+        sent += write(g, T, topo, core, ring(-4), T["fc"][:, halves[h]], T["fa"][:, halves[h]], "ac%d" % h)
+    sent += write(g, T, topo, core, ring(-2), T["fb"][:], T["fa"][:], "ab")
     W("v", k_w)
     W("s", k_w)
     kd = []
     for h in range(2):
-        fa = T["fa%d" % h]
-        k = inc(lists(fa[:], h, kq))
-        W("g", k)
-        sent += write(g, T, topo, core, ring(2), T["fb%d" % h][:], fa[:], "ag%d" % h)
-        W("v", k)
-        W("s", k)
-        kd.append(gather(wd, 16 + 1024 * h, vr[:], fa, 0, 480))
+        R("vs", "ac%d" % h)
+        kd.append(gather(wd, 16 + 1024 * h, vr[:], "fc", h))
     W("t", k_k, k_as)
     for h in range(2):
         W("t", kd[h])
-        k_x = inc(wrap(psa[:, 64 * h:64 * h + 64], "bases", wd, 16 + 1024 * h), None if h == 0 else k_x)
+        k_x = inc(wrap(psa[:, halves[h]], "bases", wd, 16 + 1024 * h), None if h == 0 else k_x)
     W("v", *kd)
     W("s", *kd)
     R("t", "at")
+    R("vs", "ab")
     kw = []
     for h in range(2):
-        R("vs", "ag%d" % h)
-        kr = gather(T["rr"], 1024 * h, wd[:], T["fb%d" % h], 0, 544)
+        kr = gather(T["rr"], 1024 * h, wd[:], "fb", h, 480)
         if h == 0:
-            W("s", k_x)
-            k_xu = inc(s.activation(T["xsum"][:], psa[:, 0:128], AF.Copy))
+            W("v", k_x)
+            k_xu = inc(v.tensor_scalar(T["xsum"][:], psa[:, 0:128], 0.0, None, OP.max))
             W("g", k_xu)
             sent += write(g, T, topo, core, ring(2), T["xt"][:], T["xsum"][:], "as")
-        t.matmul(pws[h][:, 0:64], T["ids"][:], T["at"][:, 64 * h:64 * h + 64], False, False)
+        t.matmul(pws[h][:, 0:64], T["ids"][:], T["at"][:, halves[h]], False, False)
         W("t", kr)
         kw.append(inc(wrap(pws[h][:, 0:64], "bases", T["rr"], 1024 * h, 1024, False, True)))
 
     kt, sc1 = T["kt"], T["sc1"]
-    k_kt = tok()
+    k_s0 = tok()
     for h in range(2):
         W("v", kw[h])
-        inc(v.tensor_scalar(kt[:, 64 * h:64 * h + 64], pws[h][:, 0:64], 0.0, None, OP.is_ge), k_kt)
-    W("v", k_kt)
+        k_kt = inc(v.tensor_scalar(kt[:, halves[h]], pws[h][:, 0:64], 0.0, None, OP.is_ge))
+        W("s", k_kt)
+        inc(s.activation(T["sum0"][:, halves[h]], pws[h][:, 0:64], AF.Copy), k_s0)
+        W("v", k_kt)
     k_scan = inc(v.tensor_tensor_scan(sc1[:, 16:144], kt[:], kt[:], 0.0, OP.add, OP.max))
     W("t", k_scan, k_c, k_xu)
     k4 = inc(t.matmul(T4, sc1[:, 16:144], T["bo16"][:], False, True))
@@ -340,27 +316,27 @@ def rank_program(g, core, T, topo):
     W("s", k1)
     inc(s.activation(T["aa"][:], T1, AF.Identity, bias=192.0 - 0.46875), k_ab)
     W("t", k_ab)
-    for a in range(4):
-        c = slice(32 * a, 32 * a + 32)
-        t.matmul(T["py"][c, 0:32], T["half"][:], T["sg"][:, c], True, False)
-        t.matmul(T["py"][c, 0:32], T["aa"][:, c], T["ee"][:, c], False, False)
-        op = t.matmul(T["py"][c, 0:32], T["nfl"][:, c], T["ee"][:, c], False, True)
+    for a in range(0, 128, 32):
+        for n in (32, 16):
+            c, d = slice(a, a + n), slice(a + n - 16, a + n)
+            t.matmul(T["py"][c, 0:16], T["half"][:, 0:n], T["sg"][:, d], True, False)
+            t.matmul(T["py"][c, 0:16], T["aa"][:, c], T["ee"][:, d], False, False)
+            op = t.matmul(T["py"][c, 0:16], T["nfl"][:, c], T["ee"][:, d], False, True)
     k_cm = inc(op)
     W("v", k_pos)
     k_pk = inc(v.tensor_tensor(T["posk"][:, 0:128], T["px"][:, 0:128], kt[:], OP.mult))
-    R("v", "as")
-    for h in range(2):
-        inc(v.tensor_tensor(T["sumw"][:, 64 * h:64 * h + 64], pws[h][:, 0:64], T["xt"][:, 64 * h:64 * h + 64], OP.add), k_pk)
+    W("t", k_s0)
+    t.matmul(T1, T["id32"][:], T["sum0"][:], True, False)
+    R("t", "as")
+    W("s", inc(t.matmul(T1, T["id16"][:], T["xt"][:], False, True)))
+    k_sum = inc(s.activation(T["sumw"][:, 0:128], T1, AF.Copy))
     W("v", k_cm, k_m)
-    k1 = inc(v.tensor_tensor(T["cmm"][:], CM, T["msk"][:], OP.mult))
-    W("v", k1)
-    k2 = inc(v.tensor_tensor(T["lf"][:], T["cmm"][:, 0:16], T["cmm"][:, 16:32], OP.add))
-    W("v", k2)
-    k3 = inc(v.tensor_scalar(T["lst"][:], T["lf"][:], 64.0, None, OP.add))
+    k3 = inc(v.tensor_scalar(T["lst"][:], CM, 64.0, None, OP.add))
     W("v", k3, k_pk)
     k_oh = inc(v.tensor_tensor(T["oh"][:], T["posk"][:].indirect(T["lst"][:]), T["m1"][:], OP.is_equal))
     W("v", k_oh)
     k_vn = inc(v.tensor_tensor(T["vn"][:], T["nam"][:].indirect(T["lst"][:]), T["oh"][:], OP.mult))
+    W("v", k_sum)
     k_vs = inc(v.tensor_tensor(T["vs"][:], T["sumw"][:].indirect(T["lst"][:]), T["oh"][:], OP.mult))
     ky = []
     for out, sel, val, k in (("py", "of", "vn", k_vn), ("px", "oh16", "vs", k_vs)):

@@ -7,33 +7,39 @@ def _sb(n, dt="bfloat16"):
 
 
 SCRATCH = {
-    "rln": _sb(128, "uint16"), "rlf": _sb(128, "uint16"), "rlt": _sb(128), "rlq": ("dram", [128, 128], "bfloat16"),
+    "rln": _sb(128, "uint16"), "rlf": _sb(128, "uint16"), "rlt": _sb(128),
     "owi": _sb(128, "int32"), "nxi": _sb(128, "int32"), "pti": _sb(128, "int32"),
     "own16": _sb(128, "uint16"), "nxt16": _sb(128, "uint16"), "pt0": _sb(128), "nx": _sb(128, "uint16"), "pt4": _sb(128),
     "tab": _sb(8192), "vr": _sb(2064), "gr": _sb(2064), "xg": _sb(2048), "wd": _sb(2064), "rr": _sb(2048),
     "f": _sb(128, "uint16"), "fi": _sb(128, "uint16"), "fa": _sb(128, "uint16"), "fb": _sb(128, "uint16"), "fc": _sb(128, "uint16"),
     "as": _sb(128), "at": _sb(128), "xsum": _sb(128, "float16"), "xt": _sb(128, "float16"),
-    "xp": ("dram", [128, 128], "bfloat16"), "pq": ("dram", [128, 128], "bfloat16"),
-    "lo": _sb(256), "m1": _sb(256), "hi": _sb(256), "ip": _sb(1, "int32"), "pf": _sb(1, "float32"), "gb": _sb(1),
-    "off": _sb(1, "float32"), "gi": _sb(1, "int32"), "gp": _sb(1, "float32"), "gq": _sb(1, "float32"),
-    "zz": _sb(144), "on": _sb(128), "half": _sb(32), "basef": _sb(144), "bases": _sb(144), "base0": _sb(144),
-    "ids": _sb(128), "id16": _sb(128, "float16"), "id32": _sb(128, "float32"), "jg": _sb(128), "bo": _sb(128), "tri": _sb(128),
+    "lo": _sb(256), "m1": _sb(256), "hi": _sb(256), "pf": _sb(1, "float32"), "gb": _sb(1),
+    "off": _sb(1, "float32"), "gq": _sb(1, "float32"),
+    "zz": _sb(144), "on": _sb(128), "half": _sb(128), "basef": _sb(144), "bases": _sb(144), "base0": _sb(144),
+    "ids": _sb(128), "id16": _sb(128, "float16"), "id32": _sb(128, "float32"), "jg": _sb(128), "bo": _sb(128),
+    "tri": _sb(128), "trj": _sb(128),
     "bo16": _sb(128), "kc": _sb(128), "cp": _sb(128), "ck": _sb(128), "c47": _sb(128),
     "of": _sb(36, "float32"), "oh16": _sb(36, "float16"), "nam": _sb(144, "float32"),
-    "kt": _sb(128), "sc1": _sb(144), "sum0": _sb(128, "float32"), "sumw": _sb(144, "float32"), "posk": _sb(144),
-    "aa": _sb(128), "nfl": _sb(128), "ee": _sb(128), "sg": _sb(128),
+    "sc1": _sb(144), "sum0": _sb(128, "float32"), "sumw": _sb(144, "float32"), "posk": _sb(144),
+    "aa": _sb(128), "ble": _sb(128), "ee": _sb(128), "sg": _sb(128),
     "lst": _sb(16, "uint16"), "oh": _sb(256), "vs": _sb(256, "float16"), "vn": _sb(256, "float32"),
     "yks": _sb(64, "float32"), "yss": _sb(64, "float32"),
     "psa": ("psum", [128, 2048], "float32"), "pwa": ("psum", [128, 512], "float32"), "pwb": ("psum", [128, 512], "float32"),
     "px": ("psum", [128, 512], "float32"), "py": ("psum", [128, 512], "float32"),
 }
-NTOK = 128
-SEMAPHORES = ["t%d" % _k for _k in range(NTOK)] + ["anx", "rn", "rf0", "rf1", "rq", "rt", "lc", "af0", "af1", "aq", "at", "ap",
-                                                   "ab", "ac0", "ac1", "as"]
+PIECES = (0, 44, 88, 128)
+ROWS = (88, 40)
+for _k, _n in enumerate(ROWS):
+    for _b in ("xp", "rlq", "pq"):
+        SCRATCH[_b + str(_k)] = ("dram", [128, _n], "bfloat16")
+NTOK = 120
+SEMAPHORES = (["t%d" % _k for _k in range(NTOK)] + ["an0", "an1", "rn0", "rn1", "rt", "lc", "at", "ap", "ab0", "ab1", "as"]
+              + [_n + str(_k) for _n in ("rf", "af", "ac", "rq", "aq") for _k in range(3)])
 
-NONE = -2048
+NONE = -2 ** 23
+UNIT = 2.0 ** -23
 ROUND = 12582912.0
-FILL_V, FILL_D, FILL_G = 3328, 1024, 320
+FILL_V, FILL_D, FILL_G = 2176, 2560, 256
 
 
 def engs(topo, src, dst, a, b):
@@ -48,8 +54,10 @@ def write(g, T, topo, src, dst, out, in_, sem, a=0, b=8):
     return k
 
 
-HANDED = (("rn", 8, "rln", 0, 128, 1, "nx", "anx"), ("rf0", 16, "rlf", 0, 64, 1, "fi", "af0"), ("rf1", 16, "rlf", 64, 128, 1, "fi", "af1"),
-          ("rq", 8, "rlq", 0, 128, -5, "pq", "aq"), ("rt", 8, "rlt", 0, 128, -1, "at", "at"))
+HANDED = ([("rn%d" % _k, 8, "rln", 64 * _k, 64 * _k + 64, 1, "nx", "an%d" % _k) for _k in range(2)]
+          + [("rf%d" % _k, 16, "rlf", PIECES[_k], PIECES[_k + 1], 1, "fi", "af%d" % _k) for _k in range(len(PIECES) - 1)]
+          + [("rq%d" % _k, 8, "rlq%d" % _k, 0, _n, -5, "pq%d" % _k, "aq%d" % _k) for _k, _n in enumerate(ROWS)]
+          + [("rt", 8, "rlt", 0, 128, -1, "at", "at")])
 
 
 def helper(T, topo, rc):
@@ -113,226 +121,246 @@ def rank_program(g, core, T, topo):
     k_hi = inc(g.iota(T["hi"][0:64, :], [[1, 2], [0, 128]], 0, 2, **small))
     a_g = 8192 - FILL_G
     a_d, a_v = a_g - FILL_V - FILL_D, a_g - FILL_V
-    k_fg = inc(g.iota(tab[:, a_g:8192], [[0, FILL_G]], NONE, 0, **small))
+    k_fill = inc(g.iota(tab[:, a_g:8192], [[0, FILL_G]], NONE, 0, **small))
     k_f0 = inc(v.memset(tab[:, 0:512], float(NONE)))
-    k_f1 = inc(v.memset(tab[:, 512:1024], float(NONE)))
-    W("y", k_f0, k_f1)
-    k_fd = inc(g.sync.dma_start(tab[:, a_d:a_v], tab[:, 0:FILL_D]), None, 16)
+    k_f1 = inc(v.memset(tab[:, 512:1280], float(NONE)))
+    W("y", k_f0)
+    inc(g.sync.dma_start(tab[:, a_d:a_d + 512], tab[:, 0:512]), k_fill, 16)
+    W("y", k_f1)
+    for a in range(a_d + 512, a_v, 1280):
+        n = min(1280, a_v - a)
+        inc(g.sync.dma_start(tab[:, a:a + n], tab[:, 0:n]), k_fill, 16)
     W("s", k_f0)
-    k_f2 = inc(s.activation(tab[:, 1024:1536], tab[:, 0:512], AF.Copy))
-    k_fill = inc(v.memset(tab[:, a_v:a_v + 512], float(NONE)))
+    k_f2 = inc(s.activation(tab[:, 1280:1792], tab[:, 0:512], AF.Copy))
     W("v", k_lo)
-    W("s", k_lo)
-    k_vr = tok()
-    for b in range(1, 8):
-        out = vr[:, 16 + 256 * b:272 + 256 * b]
-        inc(v.tensor_copy(out, vr[:, 16:272]) if b <= 5 else s.activation(out, vr[:, 16:272], AF.Copy), k_vr)
+    k1 = inc(v.tensor_copy(vr[:, 272:528], vr[:, 16:272]))
+    W("v", k1)
+    k_vr = inc(v.tensor_copy(vr[:, 528:1040], vr[:, 16:528]))
+    inc(v.tensor_copy(vr[:, 1040:1552], vr[:, 16:528]), k_vr)
+    W("s", k1)
+    inc(s.activation(vr[:, 1552:2064], vr[:, 16:528], AF.Copy), k_vr)
     W("y", k_vr, k_hi)
-    k_vp = inc(g.sync.dma_start(vr[0:128:16, 16:2064], T["hi"][0:64, :]), None, 16)
+    inc(g.sync.dma_start(vr[0:128:16, 16:2064], T["hi"][0:64, :]), k_fill, 16)
     W("s", k_f1, k_f2)
-    for a in range(1536, a_d, 1536):
-        n = min(1536, a_d - a)
-        inc(s.activation(tab[:, a:a + n], tab[:, 0:n], AF.Copy), k_fill)
-    inc(v.memset(tab[:, a_v + 512:a_v + 896], float(NONE)), k_fill)
+    inc(s.activation(tab[:, 1792:a_d], tab[:, 0:a_d - 1792], AF.Copy), k_fill)
     W("v", l_pt)
     k_p0 = inc(v.tensor_copy(T["pt0"][:], T["pti"][:]))
     W("y", k_p0)
-    inc(g.sync.dma_start(vr[4:128:16, 16:2064], T["pt0"][:]), k_vp, 16)
+    inc(g.sync.dma_start(vr[4:128:16, 16:2064], T["pt0"][:]), k_fill, 16)
     W("v", l_nx)
     k_n16 = inc(v.tensor_copy(T["nxt16"][:], T["nxi"][:]))
-    inc(v.memset(tab[:, a_v + 896:a_g], float(NONE)), k_fill)
+    v.memset(tab[:, a_v:a_g], float(NONE))
     W("v", l_ow)
-    k_o16 = inc(v.tensor_copy(T["own16"][:], T["owi"][:]))
-    W("v", k_f0, k_f1, k_f2, k_fill, k_fd, k_fg, k_vp, k_o16)
+    inc(v.tensor_copy(T["own16"][:], T["owi"][:]), k_fill)
+    W("v", k_fill)
     k_tab = inc(v.tensor_copy(tab[:, 0:8192].indirect(T["own16"][:, 0:128]), vr[:, 16:2064]))
 
     H = helper(T, topo, core)
     W("g", k_n16)
-    sent = write(g, T, topo, core, H, T["rln"][:], T["nxt16"][:], "rn", 8, 16)
+    halves = (slice(0, 64), slice(64, 128))
+    sent = [0]
+
+    def send(dst, out, in_, sem, a=0, b=8):
+        sent[0] += write(g, T, topo, core, dst, out, in_, sem, a, b)
+
+    for h in range(2):
+        send(H, T["rln"][:, halves[h]], T["nxt16"][:, halves[h]], "rn%d" % h, 8, 16)
     k_pf = inc(g.iota(T["pf"][:], [[0, 1]], 0, 1, **small))
     k_z = inc(g.iota(T["zz"][:], [[0, 144]], 0, 0, **small))
     W("g", k_z)
     kb = inc(g.affine_select(T["basef"][:], T["zz"][:], [[-512, 9], [1, 16]], OP.not_equal, 128.0, -15, 32))
-    k_b0 = inc(g.affine_select(T["base0"][:], T["zz"][:], [[-512, 9], [1, 16]], OP.not_equal, 1.0, -143, 32))
+    k_b0 = inc(g.affine_select(T["base0"][:], T["zz"][:], [[-512, 9], [1, 16]], OP.not_equal, UNIT, -143, 32))
     W("g", kb)
     k_bf = inc(g.affine_select(T["basef"][:], T["basef"][:], [[-512, 9], [1, 16]], OP.not_equal, 1.0, -271, 32))
     W("g", k_p0)
-    sent += write(g, T, topo, core, ring(-4), T["pt4"][:], T["pt0"][:], "ap")
+    send(ring(-4), T["pt4"][:], T["pt0"][:], "ap")
     k_lo = inc(g.iota(T["lo"][:], [[1, 256]], 0, 0, **small))
-    k_j = inc(g.iota(T["ip"][:], [[0, 1]], 0, 1))
-    inc(g.iota(T["jg"][:], [[1, 8], [0, 16]], 0, 0, **small), k_j)
-    inc(g.iota(T["kc"][:], [[0, 8], [1, 16]], 0, 0, **small), k_j)
+    k_j = inc(g.iota(T["kc"][:], [[0, 8], [1, 16]], 0, 0, **small))
     W("s", k_pf)
-    W("s", inc(s.activation(T["gb"][:], T["pf"][:], AF.Identity, scale=1.0 / 16, bias=192.0 - 0.46875)))
+    k_gb = inc(s.activation(T["gb"][:], T["pf"][:], AF.Identity, scale=1.0 / 16, bias=192.0 - 0.46875))
+    W("s", k_gb)
     k_off = inc(s.activation(T["off"][:], T["gb"][:], AF.Identity, scale=-2048.0, bias=192.0 * 2048 + 16))
+    k_c = inc(s.activation(T["gq"][:], T["gb"][:], AF.Identity, scale=4.0, bias=3.0 - 4 * 192))
+    W("s", k_z)
+    for name, a, n, val in (("gr", 0, 16, NONE), ("vr", 0, 16, NONE // 2), ("wd", 0, 16, NONE // 2), ("sumw", 128, 16, 0),
+                            ("posk", 128, 16, 1), ("nam", 128, 16, 0), ("sc1", 0, 16, 128), ("on", 0, 128, 1),
+                            ("half", 0, 128, 0.5), ("c47", 0, 128, -15.0 / 4096)):
+        inc(s.activation(T[name][:, a:a + n], T["zz"][:, 0:n], AF.Identity, bias=float(val)), k_c)
 
     pws = (T["pwa"], T["pwb"])
     pqs = (T["px"], T["py"])
-    halves = (slice(0, 64), slice(64, 128))
 
     def wrap(out, base, row, a, n=1024, first=True, last=True):
         for p in range(16):
             op = t.matmul(out, T[base][:, 15 - p:143 - p], row[:, a + p:a + n:16], first and p == 0, last and p == 15)
         return op
 
-    def lists(out, h, kws):
-        W("v", kws[h])
-        return inc(v.tensor_scalar(T[out][:, halves[h]], pqs[h][:, 0:64], T["off"][:, 0:1], 0.0, OP.add, OP.max))
+    def gather(out, a, win, lst, c, d, less=0):
+        m = (c + d) // 2 - less
+        k = inc(v.tensor_copy(out[:, a + 16 * c:a + 16 * m], win.indirect(T[lst][:, c:m])))
+        return inc(s.activation(out[:, a + 16 * m:a + 16 * d], win.indirect(T[lst][:, m:d]), AF.Copy), k)
 
-    def gather(out, a, win, lst, h, nv=512):
-        c = 64 * h
-        k = inc(v.tensor_copy(out[:, a:a + nv], win.indirect(T[lst][:, c:c + nv // 16])))
-        return inc(s.activation(out[:, a + nv:a + 1024], win.indirect(T[lst][:, c + nv // 16:c + 64]), AF.Copy), k)
+    def compose(out, a, win, lst, arrivals, made, go, less):
+        kg, kw, kl = [], [], []
 
-    W("t", k_b0, k_vp)
+        def finish(j):
+            c, d = PIECES[j], PIECES[j + 1]
+            W("v", k_off, kw[j])
+            kl.append(inc(v.tensor_scalar(T[made][:, c:d], pqs[j % 2][:, 0:d - c], T["off"][:, 0:1], 0.0, OP.add, OP.max)))
+            W("g", kl[j])
+            go(j, slice(c, d))
+
+        for j in range(len(PIECES) - 1):
+            c, d = PIECES[j], PIECES[j + 1]
+            if j < len(arrivals):
+                R("vs", arrivals[j])
+            kg.append(gather(out, a, win, lst, c, d, less if j > 1 else 0))
+            W("t", *kl[:max(j - 1, 0)], kg[j])
+            kw.append(inc(wrap(pqs[j % 2][:, 0:d - c], "basef", out, a + 16 * c, 16 * (d - c))))
+            if j > 0:
+                finish(j - 1)
+        finish(len(PIECES) - 2)
+        return kg, kl
+
+    W("t", k_b0, k_fill)
     for h in range(2):
         k_pw = inc(wrap(pws[h][:, 0:64], "base0", vr, 16 + 1024 * h, 1024, True, False), None if h == 0 else k_pw)
 
-    R("vs", "anx")
-    W("v", k_tab, k_off)
+    W("v", k_tab)
     W("s", k_tab)
-    kg = [gather(gr, 16 + 1024 * h, tab[:, 0:8192], "nx", h) for h in range(2)]
-    W("y", *kg)
-    k_xs = inc(g.sync.dma_start(T["xp"][:], gr[4:128:16, 16:2064]), None, 16)
     W("t", k_bf)
-    kw = []
-    for h in range(2):
-        W("t", kg[h])
-        kw.append(inc(wrap(pqs[h][:, 0:64], "basef", gr, 16 + 1024 * h)))
+    kg, k_f = compose(gr, 16, tab[:, 0:8192], "nx", ("an0", "an1"), "f",
+                      lambda j, c: send(H, T["rlf"][:, c], T["f"][:, c], "rf%d" % j, 0, 16), 4)
     k_aw = inc(wrap(psa[:, 0:128], "base0", gr, 16, 2048))
-    k_f = [lists("f", h, kw) for h in range(2)]
+    cuts = [16 + 16 * sum(ROWS[:j]) for j in range(len(ROWS) + 1)]
+    for j in range(len(ROWS)):
+        W("y", kg[j - len(ROWS)])
+        W("g", inc(g.sync.dma_start(T["xp%d" % j][:], gr[4:128:16, cuts[j]:cuts[j + 1]]), None, 16))
+        send(H, T["rlq%d" % j][:], T["xp%d" % j][:], "rq%d" % j, 8, 16)
 
-    for h in range(2):
-        W("g", k_f[h])
-        sent += write(g, T, topo, core, H, T["rlf"][:, halves[h]], T["f"][:, halves[h]], "rf%d" % h, 0, 16)
-    W("g", k_xs)
-    sent += write(g, T, topo, core, H, T["rlq"][:], T["xp"][:], "rq", 8, 16)
-
-    W("s", k_lo)
-    k_c = tok()
-    for name, a, val in (("gr", 0, NONE), ("vr", 0, NONE), ("wd", 0, NONE), ("sumw", 128, 0), ("posk", 128, 0), ("nam", 128, 0), ("sc1", 0, 0)):
-        inc(s.activation(T[name][:, a:a + 16], T["lo"][:, 0:16], AF.Identity, bias=float(val), scale=0.0), k_c)
     W("s", k_pw)
     R("s", "ap")
     k_w = inc(g.scalar.dma_start(vr[0:128:16, 16:2064], T["pt4"][:]), None, 16)
+    W("s", k_lo, k_j)
+    k_jg = inc(s.activation(T["jg"][:], T["lo"][:, 0:128], AF.Identity, scale=1.0 / 16, bias=192.0 - 0.46875))
+    k_m = inc(s.activation(T["m1"][:], T["lo"][:], AF.Identity, bias=-255.0))
+    k_sc = inc(s.activation(T["cp"][:], T["kc"][:], AF.Identity, scale=-1.0 / 2048))
+    inc(s.activation(T["ck"][:], T["kc"][:], AF.Copy, scale=-1.0 / 128), k_sc)
     W("s", k_aw)
-    k_as = inc(s.activation(T["as"][:], psa[:, 0:128], AF.Copy))
+    k_as = inc(s.activation(T["as"][:], psa[:, 0:128], AF.Relu, scale=1 / UNIT))
     W("g", k_as)
-    sent += write(g, T, topo, core, H, T["rlt"][:], T["as"][:], "rt", 8, 16)
+    send(H, T["rlt"][:], T["as"][:], "rt", 8, 16)
     W("y", k_pw)
-    R("y", "aq")
-    inc(g.sync.dma_start(vr[8:128:16, 16:2064], T["pq"][:]), k_w, 16)
+    for j in range(len(ROWS)):
+        R("y", "aq%d" % j)
+        inc(g.sync.dma_start(vr[8:128:16, cuts[j]:cuts[j + 1]], T["pq%d" % j][:]), k_w, 16)
 
-    W("v", k_j, k_lo, k_pf)
-    k1 = inc(v.tensor_scalar(T["gi"][:], T["ip"][:], 4, None, OP.arith_shift_right))
-    k_on = inc(v.memset(T["on"][:], 1.0))
-    k_k = inc(v.tensor_scalar(T["bases"][:], T["basef"][:], 0.0, None, OP.is_gt))
-    W("v", k1)
-    k2 = inc(v.tensor_copy(T["gp"][:], T["gi"][:]))
-    inc(v.tensor_scalar(T["gq"][:], T["gi"][:], 4.0, 3.0, OP.mult, OP.add), k2)
-    for name in ("ids", "id16", "id32"):
+    W("v", k_lo, k_pf, k_c, k_gb)
+    k_k = inc(v.tensor_scalar(T["bases"][:], T["basef"][:], 0.0, UNIT, OP.is_gt, OP.mult))
+    inc(v.tensor_scalar(T["ids"][:], T["lo"][:, 0:128], T["pf"][:, 0:1], UNIT, OP.is_equal, OP.mult), k_k)
+    for name in ("id16", "id32"):
         inc(v.tensor_scalar(T[name][:], T["lo"][:, 0:128], T["pf"][:, 0:1], None, OP.is_equal), k_k)
-    W("v", k2)
-    k_bo = inc(v.tensor_scalar(T["bo"][:], T["jg"][:], T["gp"][:, 0:1], None, OP.is_equal))
     for name in ("of", "oh16"):
         inc(v.tensor_scalar(T[name][:], T["lo"][:, 0:36], T["gq"][:, 0:1], None, OP.is_equal), k_k)
-    k_m = inc(v.tensor_scalar(T["m1"][:], T["lo"][:], 1.0, None, OP.add))
     inc(v.tensor_scalar(T["nam"][:, 0:128], T["owi"][:], 1.0, None, OP.add), k_m)
-    W("g", k_bo)
-    inc(g.affine_select(T["tri"][:], T["bo"][:], [[1, 128]], OP.is_ge, 0.0, 0, -1), k_k)
-    W("s", k_on, k_j, k_bo)
-    k_sc = inc(s.activation(T["cp"][:], T["kc"][:], AF.Identity, scale=-2.0 / 4096, bias=-17.0 / 4096))
-    inc(s.activation(T["ck"][:], T["kc"][:], AF.Copy, scale=-1.0 / 128), k_sc)
-    inc(s.activation(T["c47"][:], T["on"][:], AF.Copy, scale=-15.0 / 4096), k_sc)
-    inc(s.activation(T["bo16"][:], T["bo"][:], AF.Copy, scale=1.0 / 16), k_sc)
-    inc(s.activation(T["half"][:], T["on"][:, 0:32], AF.Copy, scale=0.5), k_sc)
-    T1, T2, T3, T4, CM = psa[:, 0:128], psa[:, 512:640], psa[:, 1024:1152], psa[:, 1536:1664], T["py"][:, 0:16]
-    W("t", k_sc)
-    t.matmul(T2, T["on"][:], T["cp"][:], True, False)
-    t.matmul(T3, T["on"][:], T["ck"][:], True, False)
-    t.matmul(T4, T["on"][:], T["ck"][:], True, False)
-    t.matmul(T4, T["on"][:], T["c47"][:], False, False)
+    W("v", k_jg)
+    k_bo = inc(v.tensor_scalar(T["bo"][:], T["jg"][:], T["gb"][:, 0:1], None, OP.is_equal))
+    inc(v.tensor_scalar(T["bo16"][:], T["jg"][:], T["gb"][:, 0:1], 1.0 / 16, OP.is_equal, OP.mult), k_sc)
 
     W("v", k_c)
     W("s", k_c)
     W("t", *k_f)
-    kq = []
+
+    def send_f2(j, c):
+        send(ring(-4), T["fc"][:, c], T["fa"][:, c], "ac%d" % j)
+        if j > 0:
+            send(ring(-2), T["fb"][:, halves[j - 1]], T["fa"][:, halves[j - 1]], "ab%d" % (j - 1))
+
+    compose(T["xg"], 0, gr[:], "fi", ("af0", "af1", "af2"), "fa", send_f2, 2)
+    W("g", k_bo)
+    k1 = inc(g.affine_select(T["tri"][:], T["bo"][:], [[1, 128]], OP.is_ge, 0.0, 0, -1))
+    inc(g.affine_select(T["trj"][:], T["bo"][:], [[-1, 128]], OP.is_ge, 0.0, 0, 1), k1)
+    W("g", k1)
+    k_tr = inc(g.affine_select(T["tri"][:], T["tri"][:], [[1, 128]], OP.not_equal, -255.0, 0, -1))
+    inc(g.affine_select(T["trj"][:], T["trj"][:], [[1, 128]], OP.not_equal, 256.0, 0, -1), k_tr)
+    T1, T2, T3, T4, CM = psa[:, 0:128], psa[:, 512:640], psa[:, 1024:1152], psa[:, 1536:1664], T["py"][:, 0:16]
+    W("t", k_sc, k_c)
+    t.matmul(T2, T["on"][:], T["cp"][:], True, False)
+    t.matmul(T2, T["on"][:], T["half"][:], False, False)
+    t.matmul(T3, T["on"][:], T["ck"][:], True, False)
+    t.matmul(T4, T["on"][:], T["ck"][:], True, False)
+    t.matmul(T4, T["on"][:], T["c47"][:], False, False)
     for h in range(2):
-        R("vs", "af%d" % h)
-        W("t", gather(T["xg"], 1024 * h, gr[:], "fi", h))
-        kq.append(inc(wrap(pqs[h][:, 0:64], "basef", T["xg"], 1024 * h)))
-    for h in range(2):
-        W("g", lists("fa", h, kq))
-        sent += write(g, T, topo, core, ring(-4), T["fc"][:, halves[h]], T["fa"][:, halves[h]], "ac%d" % h)
-    sent += write(g, T, topo, core, ring(-2), T["fb"][:], T["fa"][:], "ab")
-    W("v", k_w)
+        t.matmul(pws[h][:, 0:64], T["bo16"][:], T["on"][:, 0:64], False, False)
+    W("v", k_m, k_w)
     W("s", k_w)
     kd = []
-    for h in range(2):
-        R("vs", "ac%d" % h)
-        kd.append(gather(wd, 16 + 1024 * h, vr[:], "fc", h))
+    for j in range(len(PIECES) - 1):
+        R("vs", "ac%d" % j)
+        kd.append(gather(wd, 16, vr[:], "fc", PIECES[j], PIECES[j + 1]))
     W("t", k_k, k_as)
-    for h in range(2):
-        W("t", kd[h])
-        k_x = inc(wrap(psa[:, halves[h]], "bases", wd, 16 + 1024 * h), None if h == 0 else k_x)
-    W("v", *kd)
-    W("s", *kd)
+    for j in range(len(PIECES) - 1):
+        W("t", kd[j])
+        op = wrap(psa[:, PIECES[j]:PIECES[j + 1]], "bases", wd, 16 + 16 * PIECES[j], 16 * (PIECES[j + 1] - PIECES[j]))
+    k_x = inc(op)
+    W("v", kd[-1])
+    W("s", kd[-1])
     R("t", "at")
-    R("vs", "ab")
+    W("t", k_tr)
     kw = []
     for h in range(2):
-        kr = gather(T["rr"], 1024 * h, wd[:], "fb", h, 480)
-        if h == 0:
+        R("vs", "ab%d" % h)
+        kr = gather(T["rr"], 0, wd[:], "fb", 64 * h, 64 * h + 64)
+        if h == 1:
             W("v", k_x)
-            k_xu = inc(v.tensor_scalar(T["xsum"][:], psa[:, 0:128], 0.0, None, OP.max))
+            k_xu = inc(v.tensor_scalar(T["xsum"][:], psa[:, 0:128], 1 / UNIT, 0.0, OP.mult, OP.max))
             W("g", k_xu)
-            sent += write(g, T, topo, core, ring(2), T["xt"][:], T["xsum"][:], "as")
+            send(ring(2), T["xt"][:], T["xsum"][:], "as")
         t.matmul(pws[h][:, 0:64], T["ids"][:], T["at"][:, halves[h]], False, False)
         W("t", kr)
         kw.append(inc(wrap(pws[h][:, 0:64], "bases", T["rr"], 1024 * h, 1024, False, True)))
 
-    kt, sc1 = T["kt"], T["sc1"]
+    sc1 = T["sc1"]
     k_s0 = tok()
     for h in range(2):
         W("v", kw[h])
-        k_kt = inc(v.tensor_scalar(kt[:, halves[h]], pws[h][:, 0:64], 0.0, None, OP.is_ge))
-        W("s", k_kt)
-        inc(s.activation(T["sum0"][:, halves[h]], pws[h][:, 0:64], AF.Copy), k_s0)
-        W("v", k_kt)
-    k_scan = inc(v.tensor_tensor_scan(sc1[:, 16:144], kt[:], kt[:], 0.0, OP.add, OP.max))
-    W("t", k_scan, k_c, k_xu)
+        k_scan = inc(v.tensor_tensor_scan(sc1[:, 16 + 64 * h:80 + 64 * h], pws[h][:, 0:64], T["zz"][:, 0:64],
+                                          sc1[:, 15 + 64 * h:16 + 64 * h], OP.add, OP.max))
+        W("s", k_scan)
+        inc(s.activation(T["sum0"][:, halves[h]], pws[h][:, 0:64], AF.Identity, scale=1 / UNIT, bias=-1 / UNIT), k_s0)
+        W("v", k_scan)
+    W("t", k_xu, k_scan)
+    k1 = inc(t.matmul(T1, sc1[:, 16:144], T["bo16"][:], True, True))
     k4 = inc(t.matmul(T4, sc1[:, 16:144], T["bo16"][:], False, True))
     k3 = inc(t.matmul(T3, sc1[:, 16:144], T["bo16"][:], False, True))
     k2 = inc(t.matmul(T2, sc1[:, 16:144], T["bo16"][:], False, True))
-    k1 = inc(t.matmul(T1, sc1[:, 16:144], T["bo16"][:], True, True))
-    t.matmul(T["px"][:, 0:128], T["bo"][:], sc1[:, 15:143], True, False)
-    k_pos = inc(t.matmul(T["px"][:, 0:128], T["tri"][:], kt[:], False, True))
-    W("v", k4)
-    k_ab = inc(v.tensor_scalar(T["ee"][:], T4, ROUND, ROUND, OP.add, OP.is_equal))
-    W("s", k3)
-    inc(s.activation(T["sg"][:], T3, AF.Sign, bias=-0.03125, scale=-1.0), k_ab)
-    W("v", k2)
-    inc(v.tensor_scalar(T["nfl"][:], T2, -1.0, -192.0, OP.mult, OP.add), k_ab)
+    t.matmul(T["px"][:, 0:128], T["trj"][:], sc1[:, 15:143], True, False)
+    k_pos = inc(t.matmul(T["px"][:, 0:128], T["tri"][:], sc1[:, 16:144], False, True))
     W("s", k1)
-    inc(s.activation(T["aa"][:], T1, AF.Identity, bias=192.0 - 0.46875), k_ab)
+    k_aa = inc(s.activation(T["aa"][:], T1, AF.Identity, bias=64 - 0.46875))
+    W("v", k4)
+    k_ab = inc(v.tensor_scalar(T["ee"][:], T4, ROUND, ROUND + 128, OP.add, OP.is_equal))
+    W("s", k3)
+    inc(s.activation(T["sg"][:], T3, AF.Sign, bias=128 - 0.03125, scale=-1.0), k_ab)
+    W("v", k2, k_aa)
+    inc(v.tensor_tensor(T["ble"][:], T2, T["aa"][:], OP.is_le), k_ab)
     W("t", k_ab)
     for a in range(0, 128, 32):
         for n in (32, 16):
             c, d = slice(a, a + n), slice(a + n - 16, a + n)
             t.matmul(T["py"][c, 0:16], T["half"][:, 0:n], T["sg"][:, d], True, False)
-            t.matmul(T["py"][c, 0:16], T["aa"][:, c], T["ee"][:, d], False, False)
-            op = t.matmul(T["py"][c, 0:16], T["nfl"][:, c], T["ee"][:, d], False, True)
+            op = t.matmul(T["py"][c, 0:16], T["ble"][:, c], T["ee"][:, d], False, True)
     k_cm = inc(op)
     W("v", k_pos)
-    k_pk = inc(v.tensor_tensor(T["posk"][:, 0:128], T["px"][:, 0:128], kt[:], OP.mult))
+    v.tensor_scalar(T["posk"][:, 0:128], T["px"][:, 0:128], -2048.0, None, OP.add)
     W("t", k_s0)
     t.matmul(T1, T["id32"][:], T["sum0"][:], True, False)
     R("t", "as")
     W("s", inc(t.matmul(T1, T["id16"][:], T["xt"][:], False, True)))
     k_sum = inc(s.activation(T["sumw"][:, 0:128], T1, AF.Copy))
-    W("v", k_cm, k_m)
+    W("v", k_cm)
     k3 = inc(v.tensor_scalar(T["lst"][:], CM, 64.0, None, OP.add))
-    W("v", k3, k_pk)
+    W("v", k3)
     k_oh = inc(v.tensor_tensor(T["oh"][:], T["posk"][:].indirect(T["lst"][:]), T["m1"][:], OP.is_equal))
     W("v", k_oh)
     k_vn = inc(v.tensor_tensor(T["vn"][:], T["nam"][:].indirect(T["lst"][:]), T["oh"][:], OP.mult))
@@ -354,4 +382,4 @@ def rank_program(g, core, T, topo):
     o2 = inc(g.sync.dma_start(T.ys[:], T["yss"][0:32, :]), None, 16)
     W("s", o1)
     W("y", o2)
-    g.wait_ge(T.sem["lc"], sent)
+    g.wait_ge(T.sem["lc"], sent[0])

from concourse.bass import DstId, RemoteDMATransfer
from concourse.mybir import AluOpType as OP, ActivationFunctionType as AF


def _sb(n, dt="bfloat16"):
    return ("sbuf", [128, n], dt)


SCRATCH = {
    "rln": _sb(128, "uint16"), "rlf": _sb(128, "uint16"), "rlt": _sb(128),
    "owi": _sb(128, "int32"), "nxi": _sb(128, "int32"), "pti": _sb(128, "int32"),
    "own16": _sb(128, "uint16"), "nxt16": _sb(128, "uint16"), "pt0": _sb(128), "nx": _sb(128, "uint16"), "pt4": _sb(128),
    "tab": _sb(8192), "vr": _sb(2064), "gr": _sb(2064), "xg": _sb(2048), "wd": _sb(2064), "rr": _sb(2048),
    "f": _sb(128, "uint16"), "fi": _sb(128, "uint16"), "fa": _sb(128, "uint16"), "fb": _sb(128, "uint16"), "fc": _sb(128, "uint16"),
    "as": _sb(128), "at": _sb(128), "xsum": _sb(128, "float16"), "xt": _sb(128, "float16"),
    "lo": _sb(256), "m1": _sb(256), "hi": _sb(256), "pf": _sb(1, "float32"), "gb": _sb(1),
    "off": _sb(1, "float32"), "gq": _sb(1, "float32"),
    "zz": _sb(144), "on": _sb(128), "half": _sb(128), "basef": _sb(144), "bases": _sb(144), "base0": _sb(144),
    "ids": _sb(128), "id16": _sb(128, "float16"), "id32": _sb(128, "float32"), "jg": _sb(128), "bo": _sb(128),
    "tri": _sb(128), "trj": _sb(128),
    "bo16": _sb(128), "kc": _sb(128), "cp": _sb(128), "ck": _sb(128), "c47": _sb(128),
    "of": _sb(36, "float32"), "oh16": _sb(36, "float16"), "nam": _sb(144, "float32"),
    "sc1": _sb(144), "sum0": _sb(128, "float32"), "sumw": _sb(144, "float32"), "posk": _sb(144),
    "aa": _sb(128), "ble": _sb(128), "ee": _sb(128), "sg": _sb(128),
    "lst": _sb(16, "uint16"), "oh": _sb(256), "vs": _sb(256, "float16"), "vn": _sb(256, "float32"),
    "yks": _sb(64, "float32"), "yss": _sb(64, "float32"),
    "psa": ("psum", [128, 2048], "float32"), "pwa": ("psum", [128, 512], "float32"), "pwb": ("psum", [128, 512], "float32"),
    "px": ("psum", [128, 512], "float32"), "py": ("psum", [128, 512], "float32"),
}
PIECES = (0, 44, 88, 128)
ROWS = (88, 40)
for _k, _n in enumerate(ROWS):
    for _b in ("xp", "rlq", "pq"):
        SCRATCH[_b + str(_k)] = ("dram", [128, _n], "bfloat16")
NTOK = 120
SEMAPHORES = (["t%d" % _k for _k in range(NTOK)] + ["an0", "an1", "rn0", "rn1", "rt", "lc", "at", "ap", "ab0", "ab1", "as"]
              + [_n + str(_k) for _n in ("rf", "af", "ac", "rq", "aq") for _k in range(3)])

NONE = -2 ** 23
UNIT = 2.0 ** -23
ROUND = 12582912.0
FILL_V, FILL_D, FILL_G = 2176, 2560, 256


def engs(topo, src, dst, a, b):
    e = topo.engines(src, dst)[a:b]
    return sum(1 << x for x in e), len(e)


def write(g, T, topo, src, dst, out, in_, sem, a=0, b=8):
    rid, pid = topo.addr(dst, src)
    m, k = engs(topo, src, dst, a, b)
    g.remote_dma(out, in_, T.sem[sem], T.sem["lc"], pid, rid, m)
    return k


HANDED = ([("rn%d" % _k, 8, "rln", 64 * _k, 64 * _k + 64, 1, "nx", "an%d" % _k) for _k in range(2)]
          + [("rf%d" % _k, 16, "rlf", PIECES[_k], PIECES[_k + 1], 1, "fi", "af%d" % _k) for _k in range(len(PIECES) - 1)]
          + [("rq%d" % _k, 8, "rlq%d" % _k, 0, _n, -5, "pq%d" % _k, "aq%d" % _k) for _k, _n in enumerate(ROWS)]
          + [("rt", 8, "rlt", 0, 128, -1, "at", "at")])


def helper(T, topo, rc):
    q, N = T.rank_of(rc), len(T.cores)
    far = [T.cores[(q + h[5]) % N] for h in HANDED]
    return [x for x in topo.cores_of(rc) if x != rc and topo.die(x) == topo.die(rc) and all(topo.may_write(x, d) for d in far)][0]


def hand_on(g, core, T, topo):
    N = len(T.cores)
    for rc in T.cores:
        if rc in topo.cores_of(core) and core == helper(T, topo, rc):
            q, sent = T.rank_of(rc), 0
            for here, n, buf, a, b, d, out, there in HANDED:
                g.wait_ge(T.sem[here], n)
                sent += write(g, T, topo, core, T.cores[(q + d) % N], T[out][:, a:b], T[buf][:, a:b], there)
            g.wait_ge(T.sem["lc"], sent)


def rank_program(g, core, T, topo):
    q = T.rank_of(core)
    if q is None:
        hand_on(g, core, T, topo)
        return
    N = len(T.cores)
    Q = {"g": g, "v": g.vector, "s": g.scalar, "t": g.tensor, "y": g.sync}
    v, s, t = g.vector, g.scalar, g.tensor
    used, seen = [0], {}
    small = {"allow_small_or_imprecise_dtypes": True}

    def tok():
        used[0] += 1
        return [T.sem["t%d" % (used[0] - 1)], 0, used[0] - 1]

    def inc(op, k=None, n=1):
        k = k or tok()
        op.then_inc(k[0], n)
        k[1] += n
        return k

    def W(queue, *toks):
        for k in toks:
            if seen.get((queue, k[2]), -1) < k[1]:
                seen[(queue, k[2])] = k[1]
                Q[queue].wait_ge(k[0], k[1])

    def R(queues, sem, n=8):
        for x in queues:
            Q[x].wait_ge(T.sem[sem], n)

    def ring(d):
        return T.cores[(q + d) % N]

    tab, vr, gr, wd, psa = T["tab"], T["vr"], T["gr"], T["wd"], T["psa"]

    l_pt = inc(g.sync.dma_start(T["pti"][:], T.pts[:]), None, 16)
    l_nx = inc(g.sync.dma_start(T["nxi"][:], T.nxt[:]), None, 16)
    l_ow = inc(g.sync.dma_start(T["owi"][:], T.own[:]), None, 16)

    k_lo = inc(g.iota(vr[:, 16:272], [[0, 2], [1, 128]], 0, 0, **small))
    k_hi = inc(g.iota(T["hi"][0:64, :], [[1, 2], [0, 128]], 0, 2, **small))
    a_g = 8192 - FILL_G
    a_d, a_v = a_g - FILL_V - FILL_D, a_g - FILL_V
    k_fill = inc(g.iota(tab[:, a_g:8192], [[0, FILL_G]], NONE, 0, **small))
    k_f0 = inc(v.memset(tab[:, 0:512], float(NONE)))
    k_f1 = inc(v.memset(tab[:, 512:1280], float(NONE)))
    W("y", k_f0)
    inc(g.sync.dma_start(tab[:, a_d:a_d + 512], tab[:, 0:512]), k_fill, 16)
    W("y", k_f1)
    for a in range(a_d + 512, a_v, 1280):
        n = min(1280, a_v - a)
        inc(g.sync.dma_start(tab[:, a:a + n], tab[:, 0:n]), k_fill, 16)
    W("s", k_f0)
    k_f2 = inc(s.activation(tab[:, 1280:1792], tab[:, 0:512], AF.Copy))
    W("v", k_lo)
    k1 = inc(v.tensor_copy(vr[:, 272:528], vr[:, 16:272]))
    W("v", k1)
    k_vr = inc(v.tensor_copy(vr[:, 528:1040], vr[:, 16:528]))
    inc(v.tensor_copy(vr[:, 1040:1552], vr[:, 16:528]), k_vr)
    W("s", k1)
    inc(s.activation(vr[:, 1552:2064], vr[:, 16:528], AF.Copy), k_vr)
    W("y", k_vr, k_hi)
    inc(g.sync.dma_start(vr[0:128:16, 16:2064], T["hi"][0:64, :]), k_fill, 16)
    W("s", k_f1, k_f2)
    inc(s.activation(tab[:, 1792:a_d], tab[:, 0:a_d - 1792], AF.Copy), k_fill)
    W("v", l_pt)
    k_p0 = inc(v.tensor_copy(T["pt0"][:], T["pti"][:]))
    W("y", k_p0)
    inc(g.sync.dma_start(vr[4:128:16, 16:2064], T["pt0"][:]), k_fill, 16)
    W("v", l_nx)
    k_n16 = inc(v.tensor_copy(T["nxt16"][:], T["nxi"][:]))
    v.memset(tab[:, a_v:a_g], float(NONE))
    W("v", l_ow)
    inc(v.tensor_copy(T["own16"][:], T["owi"][:]), k_fill)
    W("v", k_fill)
    k_tab = inc(v.tensor_copy(tab[:, 0:8192].indirect(T["own16"][:, 0:128]), vr[:, 16:2064]))

    H = helper(T, topo, core)
    W("g", k_n16)
    halves = (slice(0, 64), slice(64, 128))
    sent = [0]

    def send(dst, out, in_, sem, a=0, b=8):
        sent[0] += write(g, T, topo, core, dst, out, in_, sem, a, b)

    for h in range(2):
        send(H, T["rln"][:, halves[h]], T["nxt16"][:, halves[h]], "rn%d" % h, 8, 16)
    k_pf = inc(g.iota(T["pf"][:], [[0, 1]], 0, 1, **small))
    k_z = inc(g.iota(T["zz"][:], [[0, 144]], 0, 0, **small))
    W("g", k_z)
    kb = inc(g.affine_select(T["basef"][:], T["zz"][:], [[-512, 9], [1, 16]], OP.not_equal, 128.0, -15, 32))
    k_b0 = inc(g.affine_select(T["base0"][:], T["zz"][:], [[-512, 9], [1, 16]], OP.not_equal, UNIT, -143, 32))
    W("g", kb)
    k_bf = inc(g.affine_select(T["basef"][:], T["basef"][:], [[-512, 9], [1, 16]], OP.not_equal, 1.0, -271, 32))
    W("g", k_p0)
    send(ring(-4), T["pt4"][:], T["pt0"][:], "ap")
    k_lo = inc(g.iota(T["lo"][:], [[1, 256]], 0, 0, **small))
    k_j = inc(g.iota(T["kc"][:], [[0, 8], [1, 16]], 0, 0, **small))
    W("s", k_pf)
    k_gb = inc(s.activation(T["gb"][:], T["pf"][:], AF.Identity, scale=1.0 / 16, bias=192.0 - 0.46875))
    W("s", k_gb)
    k_off = inc(s.activation(T["off"][:], T["gb"][:], AF.Identity, scale=-2048.0, bias=192.0 * 2048 + 16))
    k_c = inc(s.activation(T["gq"][:], T["gb"][:], AF.Identity, scale=4.0, bias=3.0 - 4 * 192))
    W("s", k_z)
    for name, a, n, val in (("gr", 0, 16, NONE), ("vr", 0, 16, NONE // 2), ("wd", 0, 16, NONE // 2), ("sumw", 128, 16, 0),
                            ("posk", 128, 16, 1), ("nam", 128, 16, 0), ("sc1", 0, 16, 128), ("on", 0, 128, 1),
                            ("half", 0, 128, 0.5), ("c47", 0, 128, -15.0 / 4096)):
        inc(s.activation(T[name][:, a:a + n], T["zz"][:, 0:n], AF.Identity, bias=float(val)), k_c)

    pws = (T["pwa"], T["pwb"])
    pqs = (T["px"], T["py"])

    def wrap(out, base, row, a, n=1024, first=True, last=True):
        for p in range(16):
            op = t.matmul(out, T[base][:, 15 - p:143 - p], row[:, a + p:a + n:16], first and p == 0, last and p == 15)
        return op

    def gather(out, a, win, lst, c, d, less=0):
        m = (c + d) // 2 - less
        k = inc(v.tensor_copy(out[:, a + 16 * c:a + 16 * m], win.indirect(T[lst][:, c:m])))
        return inc(s.activation(out[:, a + 16 * m:a + 16 * d], win.indirect(T[lst][:, m:d]), AF.Copy), k)

    def compose(out, a, win, lst, arrivals, made, go, less):
        kg, kw, kl = [], [], []

        def finish(j):
            c, d = PIECES[j], PIECES[j + 1]
            W("v", k_off, kw[j])
            kl.append(inc(v.tensor_scalar(T[made][:, c:d], pqs[j % 2][:, 0:d - c], T["off"][:, 0:1], 0.0, OP.add, OP.max)))
            W("g", kl[j])
            go(j, slice(c, d))

        for j in range(len(PIECES) - 1):
            c, d = PIECES[j], PIECES[j + 1]
            if j < len(arrivals):
                R("vs", arrivals[j])
            kg.append(gather(out, a, win, lst, c, d, less if j > 1 else 0))
            W("t", *kl[:max(j - 1, 0)], kg[j])
            kw.append(inc(wrap(pqs[j % 2][:, 0:d - c], "basef", out, a + 16 * c, 16 * (d - c))))
            if j > 0:
                finish(j - 1)
        finish(len(PIECES) - 2)
        return kg, kl

    W("t", k_b0, k_fill)
    for h in range(2):
        k_pw = inc(wrap(pws[h][:, 0:64], "base0", vr, 16 + 1024 * h, 1024, True, False), None if h == 0 else k_pw)

    W("v", k_tab)
    W("s", k_tab)
    W("t", k_bf)
    kg, k_f = compose(gr, 16, tab[:, 0:8192], "nx", ("an0", "an1"), "f",
                      lambda j, c: send(H, T["rlf"][:, c], T["f"][:, c], "rf%d" % j, 0, 16), 4)
    k_aw = inc(wrap(psa[:, 0:128], "base0", gr, 16, 2048))
    cuts = [16 + 16 * sum(ROWS[:j]) for j in range(len(ROWS) + 1)]
    for j in range(len(ROWS)):
        W("y", kg[j - len(ROWS)])
        W("g", inc(g.sync.dma_start(T["xp%d" % j][:], gr[4:128:16, cuts[j]:cuts[j + 1]]), None, 16))
        send(H, T["rlq%d" % j][:], T["xp%d" % j][:], "rq%d" % j, 8, 16)

    W("s", k_pw)
    R("s", "ap")
    k_w = inc(g.scalar.dma_start(vr[0:128:16, 16:2064], T["pt4"][:]), None, 16)
    W("s", k_lo, k_j)
    k_jg = inc(s.activation(T["jg"][:], T["lo"][:, 0:128], AF.Identity, scale=1.0 / 16, bias=192.0 - 0.46875))
    k_m = inc(s.activation(T["m1"][:], T["lo"][:], AF.Identity, bias=-255.0))
    k_sc = inc(s.activation(T["cp"][:], T["kc"][:], AF.Identity, scale=-1.0 / 2048))
    inc(s.activation(T["ck"][:], T["kc"][:], AF.Copy, scale=-1.0 / 128), k_sc)
    W("s", k_aw)
    k_as = inc(s.activation(T["as"][:], psa[:, 0:128], AF.Relu, scale=1 / UNIT))
    W("g", k_as)
    send(H, T["rlt"][:], T["as"][:], "rt", 8, 16)
    W("y", k_pw)
    for j in range(len(ROWS)):
        R("y", "aq%d" % j)
        inc(g.sync.dma_start(vr[8:128:16, cuts[j]:cuts[j + 1]], T["pq%d" % j][:]), k_w, 16)

    W("v", k_lo, k_pf, k_c, k_gb)
    k_k = inc(v.tensor_scalar(T["bases"][:], T["basef"][:], 0.0, UNIT, OP.is_gt, OP.mult))
    inc(v.tensor_scalar(T["ids"][:], T["lo"][:, 0:128], T["pf"][:, 0:1], UNIT, OP.is_equal, OP.mult), k_k)
    for name in ("id16", "id32"):
        inc(v.tensor_scalar(T[name][:], T["lo"][:, 0:128], T["pf"][:, 0:1], None, OP.is_equal), k_k)
    for name in ("of", "oh16"):
        inc(v.tensor_scalar(T[name][:], T["lo"][:, 0:36], T["gq"][:, 0:1], None, OP.is_equal), k_k)
    inc(v.tensor_scalar(T["nam"][:, 0:128], T["owi"][:], 1.0, None, OP.add), k_m)
    W("v", k_jg)
    k_bo = inc(v.tensor_scalar(T["bo"][:], T["jg"][:], T["gb"][:, 0:1], None, OP.is_equal))
    inc(v.tensor_scalar(T["bo16"][:], T["jg"][:], T["gb"][:, 0:1], 1.0 / 16, OP.is_equal, OP.mult), k_sc)

    W("v", k_c)
    W("s", k_c)
    W("t", *k_f)

    def send_f2(j, c):
        send(ring(-4), T["fc"][:, c], T["fa"][:, c], "ac%d" % j)
        if j > 0:
            send(ring(-2), T["fb"][:, halves[j - 1]], T["fa"][:, halves[j - 1]], "ab%d" % (j - 1))

    compose(T["xg"], 0, gr[:], "fi", ("af0", "af1", "af2"), "fa", send_f2, 2)
    W("g", k_bo)
    k1 = inc(g.affine_select(T["tri"][:], T["bo"][:], [[1, 128]], OP.is_ge, 0.0, 0, -1))
    inc(g.affine_select(T["trj"][:], T["bo"][:], [[-1, 128]], OP.is_ge, 0.0, 0, 1), k1)
    W("g", k1)
    k_tr = inc(g.affine_select(T["tri"][:], T["tri"][:], [[1, 128]], OP.not_equal, -255.0, 0, -1))
    inc(g.affine_select(T["trj"][:], T["trj"][:], [[1, 128]], OP.not_equal, 256.0, 0, -1), k_tr)
    T1, T2, T3, T4, CM = psa[:, 0:128], psa[:, 512:640], psa[:, 1024:1152], psa[:, 1536:1664], T["py"][:, 0:16]
    W("t", k_sc, k_c)
    t.matmul(T2, T["on"][:], T["cp"][:], True, False)
    t.matmul(T2, T["on"][:], T["half"][:], False, False)
    t.matmul(T3, T["on"][:], T["ck"][:], True, False)
    t.matmul(T4, T["on"][:], T["ck"][:], True, False)
    t.matmul(T4, T["on"][:], T["c47"][:], False, False)
    for h in range(2):
        t.matmul(pws[h][:, 0:64], T["bo16"][:], T["on"][:, 0:64], False, False)
    W("v", k_m, k_w)
    W("s", k_w)
    kd = []
    for j in range(len(PIECES) - 1):
        R("vs", "ac%d" % j)
        kd.append(gather(wd, 16, vr[:], "fc", PIECES[j], PIECES[j + 1]))
    W("t", k_k, k_as)
    for j in range(len(PIECES) - 1):
        W("t", kd[j])
        op = wrap(psa[:, PIECES[j]:PIECES[j + 1]], "bases", wd, 16 + 16 * PIECES[j], 16 * (PIECES[j + 1] - PIECES[j]))
    k_x = inc(op)
    W("v", kd[-1])
    W("s", kd[-1])
    R("t", "at")
    W("t", k_tr)
    kw = []
    for h in range(2):
        R("vs", "ab%d" % h)
        kr = gather(T["rr"], 0, wd[:], "fb", 64 * h, 64 * h + 64)
        if h == 1:
            W("v", k_x)
            k_xu = inc(v.tensor_scalar(T["xsum"][:], psa[:, 0:128], 1 / UNIT, 0.0, OP.mult, OP.max))
            W("g", k_xu)
            send(ring(2), T["xt"][:], T["xsum"][:], "as")
        t.matmul(pws[h][:, 0:64], T["ids"][:], T["at"][:, halves[h]], False, False)
        W("t", kr)
        kw.append(inc(wrap(pws[h][:, 0:64], "bases", T["rr"], 1024 * h, 1024, False, True)))

    sc1 = T["sc1"]
    k_s0 = tok()
    for h in range(2):
        W("v", kw[h])
        k_scan = inc(v.tensor_tensor_scan(sc1[:, 16 + 64 * h:80 + 64 * h], pws[h][:, 0:64], T["zz"][:, 0:64],
                                          sc1[:, 15 + 64 * h:16 + 64 * h], OP.add, OP.max))
        W("s", k_scan)
        inc(s.activation(T["sum0"][:, halves[h]], pws[h][:, 0:64], AF.Identity, scale=1 / UNIT, bias=-1 / UNIT), k_s0)
        W("v", k_scan)
    W("t", k_xu, k_scan)
    k1 = inc(t.matmul(T1, sc1[:, 16:144], T["bo16"][:], True, True))
    k4 = inc(t.matmul(T4, sc1[:, 16:144], T["bo16"][:], False, True))
    k3 = inc(t.matmul(T3, sc1[:, 16:144], T["bo16"][:], False, True))
    k2 = inc(t.matmul(T2, sc1[:, 16:144], T["bo16"][:], False, True))
    t.matmul(T["px"][:, 0:128], T["trj"][:], sc1[:, 15:143], True, False)
    k_pos = inc(t.matmul(T["px"][:, 0:128], T["tri"][:], sc1[:, 16:144], False, True))
    W("s", k1)
    k_aa = inc(s.activation(T["aa"][:], T1, AF.Identity, bias=64 - 0.46875))
    W("v", k4)
    k_ab = inc(v.tensor_scalar(T["ee"][:], T4, ROUND, ROUND + 128, OP.add, OP.is_equal))
    W("s", k3)
    inc(s.activation(T["sg"][:], T3, AF.Sign, bias=128 - 0.03125, scale=-1.0), k_ab)
    W("v", k2, k_aa)
    inc(v.tensor_tensor(T["ble"][:], T2, T["aa"][:], OP.is_le), k_ab)
    W("t", k_ab)
    for a in range(0, 128, 32):
        for n in (32, 16):
            c, d = slice(a, a + n), slice(a + n - 16, a + n)
            t.matmul(T["py"][c, 0:16], T["half"][:, 0:n], T["sg"][:, d], True, False)
            op = t.matmul(T["py"][c, 0:16], T["ble"][:, c], T["ee"][:, d], False, True)
    k_cm = inc(op)
    W("v", k_pos)
    v.tensor_scalar(T["posk"][:, 0:128], T["px"][:, 0:128], -2048.0, None, OP.add)
    W("t", k_s0)
    t.matmul(T1, T["id32"][:], T["sum0"][:], True, False)
    R("t", "as")
    W("s", inc(t.matmul(T1, T["id16"][:], T["xt"][:], False, True)))
    k_sum = inc(s.activation(T["sumw"][:, 0:128], T1, AF.Copy))
    W("v", k_cm)
    k3 = inc(v.tensor_scalar(T["lst"][:], CM, 64.0, None, OP.add))
    W("v", k3)
    k_oh = inc(v.tensor_tensor(T["oh"][:], T["posk"][:].indirect(T["lst"][:]), T["m1"][:], OP.is_equal))
    W("v", k_oh)
    k_vn = inc(v.tensor_tensor(T["vn"][:], T["nam"][:].indirect(T["lst"][:]), T["oh"][:], OP.mult))
    W("v", k_sum)
    k_vs = inc(v.tensor_tensor(T["vs"][:], T["sumw"][:].indirect(T["lst"][:]), T["oh"][:], OP.mult))
    ky = []
    for out, sel, val, k in (("py", "of", "vn", k_vn), ("px", "oh16", "vs", k_vs)):
        W("t", k)
        for a in range(4):
            op = t.matmul(T[out][0:32, 0:64], T[sel][:, 3 - a:35 - a], T[val][:, 64 * a:64 * a + 64], a == 0, a == 3)
        ky.append(inc(op))
    W("s", ky[0])
    k1 = inc(s.activation(T["yks"][0:32, :], T["py"][0:32, 0:64], AF.Identity, bias=-1.0))
    W("s", k1)
    o1 = inc(g.scalar.dma_start(T.yk[:], T["yks"][0:32, :]), None, 16)
    W("v", ky[1])
    k2 = inc(v.tensor_copy(T["yss"][0:32, :], T["px"][0:32, 0:64]))
    W("y", k2)
    o2 = inc(g.sync.dma_start(T.ys[:], T["yss"][0:32, :]), None, 16)
    W("s", o1)
    W("y", o2)
    g.wait_ge(T.sem["lc"], sent[0])
